import numpy as np, ml_dtypes
CORES = [23,119,17,113]
N = 4
import mx_ref
BF = ml_dtypes.bfloat16
def entries(a):
    return np.ascontiguousarray(a.T).reshape(-1)
def table(e):
    return np.ascontiguousarray(np.reshape(e, (-1, 16)).T).astype(np.int32)
def cols(t, e):
    v = np.concatenate([t.reshape(128, -1, 4), np.zeros((128, 1, 4), BF)], axis=1)
    return np.ascontiguousarray(v[:, e]).reshape(128, -1)
def cut(t, i, w=512):
    return t[:, w * i:w * i + w]
def f(rng, *shape):
    return mx_ref.flush((rng.standard_normal(shape, dtype=np.float32) * np.exp2(rng.integers(-2, 3, shape[:-1] + (1,)))).astype(BF))
def wide(rng, *shape, cols=0):
    v = rng.standard_normal(shape, dtype=np.float32) * np.exp2(rng.integers(-12, 13, shape)).astype(np.float32)
    if cols: v *= np.repeat(np.exp2(rng.integers(-cols, cols + 1, shape[:-2] + (1, shape[-1] // 4))) * (rng.random(shape[:-2] + (1, shape[-1] // 4)) > 0.0625), 4, axis=-1).astype(np.float32)
    return mx_ref.flush(v.astype(BF))
T, V, M, CAPP, R, O = 512, 192, 288, 64, 3, 2
START = np.repeat(np.arange(N), V)
def loose(rng, at, to, who, but=-1):
    to = to.copy(); n = np.zeros((N, N), int); np.add.at(n, (at, to), 1)
    for i in rng.permutation(who):
        q = rng.integers(0, N)
        if q != but and n[:, q].sum() < M and (q == at[i] or n[at[i], q] < CAPP): n[at[i], to[i]] -= 1; n[at[i], q] += 1; to[i] = q
    return to
def turn(rng, at):
    to = at.copy(); far = 1 + rng.permutation(N - 1)
    for s in range(N):
        k = rng.permutation(np.flatnonzero(at == s))
        for i in range(min(N - 1, len(k) // CAPP)): to[k[CAPP * i:CAPP * i + CAPP]] = (s + far[i]) % N
    return to
def collect(rng, at, e):
    to = at.copy(); k = rng.permutation(np.flatnonzero(at == e))[M - (N - 1) * CAPP:]
    to[k] = (e + 1 + np.arange(len(k)) % (N - 1)) % N
    for s in range(N):
        if s != e: to[rng.permutation(np.flatnonzero(at == s))[:CAPP]] = e
    return to
def spill(rng, at, to, who, ranks):
    to = to.copy(); n = np.zeros((N, N), int); others = np.setdiff1d(np.arange(N * V), who); np.add.at(n, (at[others], to[others]), 1)
    for i in rng.permutation(who):
        q = ranks[np.argmin(np.where(n[at[i], ranks] < CAPP, n[:, ranks].sum(axis=0), N * V))]
        n[at[i], q] += 1; to[i] = q
    return to
def lists(rng, a, share=0.25):
    nx = rng.integers(0, N * T, (N, 2 * T)); free = [list(rng.permutation(2 * T)) for r in range(N)]
    way = np.zeros((R - 1, N * V), int)
    for k in range(R - 2, -1, -1):
        goal = a[k + 1] if k == R - 2 else a[k + 1] * T + way[k + 1] // 2
        known = {}
        for i in rng.permutation(N * V):
            s = int(a[k][i]); L = known.setdefault((s, int(goal[i])), [])
            if not L or rng.random() >= share:
                L.append(free[s].pop()); way[k, i] = L[-1]
            else: way[k, i] = L[rng.integers(0, len(L))]
        if k < R - 2: nx[a[k], way[k]] = goal
    nx[a[R - 2], way[R - 2]] = a[R - 1] * T + rng.integers(0, T, N * V)
    st = (way[0] // 2).reshape(N, V); bt = sum((way[k] % 2) << k for k in range(R - 1)).reshape(N, V)
    return {"nx": np.stack([table(e) for e in nx]), "st": np.stack([table(e) for e in st]), "bt": np.stack([table(e) for e in bt])}
def setup_inputs(rng):
    a = [START]
    for k in range(R - 1): a.append(loose(rng, a[k], a[k], np.arange(N * V)))
    return {"x": f(rng, N, 128, 4 * T), "w": f(rng, N, 128, R * O * 512), **lists(rng, a)}
def setup_inputs_through(rng):
    h = rng.integers(1, N); a = [START, START.copy(), (START + h) % N]
    for s in range(N):
        for g, k in enumerate(np.array_split(V * s + rng.permutation(V), -(-V // CAPP))): a[1][k] = (s + g) % N
    return {**setup_inputs(rng), **lists(rng, a)}
def setup_inputs_far(rng):
    a = [START]
    for k in range(R - 1): a.append(turn(rng, a[k]))
    a[R - 1] = loose(rng, a[R - 2], a[R - 1], np.flatnonzero(a[R - 1] == a[R - 2]))
    return {**setup_inputs(rng), **lists(rng, a)}
def setup_inputs_gather(rng):
    p = rng.permutation(N); home, end, bare = p[:3]; a = [START, START.copy()]
    for j, s in enumerate(p[2:]): a[1][rng.permutation(np.flatnonzero(START == s))[:min(CAPP, max(0, M - V - j * CAPP))]] = home
    to = collect(rng, a[1], end)
    to = spill(rng, a[1], to, np.flatnonzero(((a[1] == end) & (to != end)) | (to == bare)), np.append(p[3:], home))
    a.append(loose(rng, a[1], to, np.flatnonzero((to == a[1]) & (a[1] != end)), but=bare))
    return {**setup_inputs(rng), **lists(rng, a, share=0.75)}
def setup_inputs_stay(rng):
    p = rng.integers(0, N); a = [START, collect(rng, START, p)]
    a.append(loose(rng, a[1], a[1], np.flatnonzero(a[1] != p)))
    return {**setup_inputs(rng), **lists(rng, a)}
def setup_inputs_spread(rng):
    d = setup_inputs(rng); d["x"] = wide(rng, N, 128, 4 * T, cols=8); return d
def follow(nx, st, bt):
    n = np.concatenate([entries(t) for t in nx]); bits = np.concatenate([entries(t) for t in bt])
    at = [np.concatenate([entries(st[r]) + r * T for r in range(N)])]
    for k in range(R - 1): at.append(n[2 * at[k] + (bits >> k & 1)])
    return at
def check_inputs(d):
    b = []
    for name, top in (("nx", N * T), ("st", T), ("bt", 2 ** (R - 1))):
        if d[name].min() < 0 or d[name].max() >= top: b.append(name)
    if b: return b
    at = [t // T for t in follow(d["nx"], d["st"], d["bt"])]
    for k in range(R):
        if np.bincount(at[k], minlength=N).max() > M: b.append("walkers on a rank at step " + str(k))
    for k in range(R - 1):
        n = np.zeros((N, N), int); np.add.at(n, (at[k], at[k + 1]), 1); np.fill_diagonal(n, 0)
        if n.max() > CAPP: b.append("walkers from a rank to another from step " + str(k))
    return b
def reference(x, w, nx, st, bt):
    nodes = np.concatenate([x[r] for r in range(N)], axis=1)
    at = follow(nx, st, bt)
    y = np.zeros((N, 128, O * M), np.float32); ids = np.full((N, 2, M), -1, np.float32)
    for e in range(N):
        m = np.flatnonzero(at[R - 1] // T == e)
        ids[e, 0, :len(m)] = m // V; ids[e, 1, :len(m)] = m % V
        for k in range(R):
            c = np.full(M, -1); c[:len(m)] = at[k][m]
            q = mx_ref.quantize(cols(nodes, c))
            for o in range(O): y[e][:, M * o:M * o + M] += mx_ref.matmul(mx_ref.quantize(np.ascontiguousarray(cut(w[e], k * O + o))), q)
    return {"y": y, "id": ids}

@@ -1,0 +1,586 @@
+from concourse.bass import DstId, RemoteDMATransfer
+from concourse.mybir import dt, AluOpType as A, ActivationFunctionType as AF
+
+N, V, M, O = 4, 192, 288, 2
+C = 64
+Z0 = 8
+X0 = Z0 + 512
+X1 = X0 + 192
+L = M // 2
+F, I, U, B = "float32", "int32", "uint16", "bfloat16"
+Q8, S8 = "float8_e4m3fn_x4", "uint8"
+
+
+def _sb(w, d):
+    return ("sbuf", [128, w], d)
+
+
+SCRATCH = {
+    "tba": _sb(1024, I), "tb": _sb(1032, F), "sb": _sb(24, I), "nxi": _sb(64, I), "nxf": _sb(64, F), "nxt": _sb(64, F),
+    "xs": _sb(4 * X0, B), "ws": _sb(3072, B),
+    "QX": _sb(X0, Q8), "SX": _sb(X0, S8), "W1": _sb(X1 + 192, Q8), "P1": _sb(X1 + 192, S8), "W2": _sb(X1 + 192, Q8), "P2": _sb(X1 + 192, S8),
+    "WQ": _sb(768, Q8), "WS": _sb(768, S8),
+    "Q1": _sb(192, Q8), "S1": _sb(192, S8), "Q3": _sb(192, Q8), "S3": _sb(192, S8), "Q4": _sb(192, Q8), "S4": _sb(192, S8),
+    "G0": _sb(288, Q8), "H0": _sb(288, S8), "G1": _sb(288, Q8), "H1": _sb(288, S8), "G2": _sb(288, Q8), "H2": _sb(288, S8),
+    "j15": _sb(192, F), "pI": _sb(1, I), "c16": _sb(12, F), "ident": _sb(1104, F), "mask": _sb(192, F), "mask2": _sb(192, F), "seg": _sb(192, F), "maskb": _sb(32, F),
+    "maskc": _sb(32, F), "sg": _sb(192, F), "ci": _sb(4, I), "cf": _sb(24, F), "i16": _sb(12, F), "park": _sb(12, F), "K2": _sb(12, F),
+    "l0": _sb(36, I), "lf": _sb(48, F), "lx": _sb(24, U), "stf": _sb(12, F),
+    "val1": _sb(192, F), "n1m": _sb(192, F), "n1s": _sb(192, F), "t1": _sb(12, I), "E1": _sb(12, F), "M1": _sb(12, U), "A1": _sb(36, U),
+    "MP": _sb(12, B), "AP": _sb(36, B),
+    "eqa": _sb(72, F), "sa": _sb(36, F), "ba": _sb(96, F), "bta": _sb(96, F), "ra": _sb(96, F), "pa": _sb(36, F), "xa": _sb(96, F),
+    "eqb": _sb(72, F), "sc": _sb(36, F), "bb": _sb(96, F), "btb": _sb(96, F), "rb": _sb(96, F), "pb": _sb(36, F), "xb": _sb(96, F), "g9": _sb(18, F),
+    "sl": _sb(36, U), "w1": _sb(384, F), "w2": _sb(384, F), "pw": _sb(480, F), "f1": _sb(384, F), "f2": _sb(384, F), "f3": _sb(288, F),
+    "stl": _sb(12, U), "off": _sb(12, U), "n2m": _sb(192, F), "n2s": _sb(192, F), "t2": _sb(12, I), "c1i": _sb(12, I), "c1u": _sb(12, U), "c1o": _sb(12, F),
+    "L0f": _sb(12, F), "L0e": _sb(12, F), "L0u": _sb(12, U), "SBm": _sb(12, F), "n2k": _sb(12, F), "M2": _sb(12, F), "A2": _sb(36, F), "uf1": _sb(192, F), "val2": _sb(192, F),
+    "hg": _sb(36, F), "fa": _sb(48, I), "l34": _sb(24, U),
+    "Zf": _sb(36, F), "Zi": _sb(48, I), "zl": _sb(24, U), "ze": _sb(24, F), "uf2": _sb(192, F), "val3": _sb(192, F), "pr": _sb(12, F), "PZ": _sb(32, F),
+    "tc": _sb(224, F), "g3": _sb(6, F), "pz": _sb(24, F), "hm": _sb(18, F), "F32": _sb(32, F), "TF": _sb(32, F), "hx": _sb(32, F), "DD": _sb(64, I), "LT": _sb(64, I),
+    "SS": _sb(32, I), "li": _sb(64, I), "LU": _sb(64, U), "HU": _sb(64, U), "idi": _sb(96, I), "idt": _sb(64, F), "ysb": _sb(576, F),
+    "ps": ("psum", [128, 2048], F),
+}
+DMAS = ["dnx", "dst", "dsu", "dx", "dx1", "dw0", "dw1", "dni", "dtr", "dtq", "dq1", "dq2", "dy0", "dy1", "di0", "di1"]
+HOPS = ("ma", "mp", "qa", "sa", "mz", "qb", "sb", "qc", "sc")
+SEMAPHORES = ["v", "s", "t", "g", "loc"] + DMAS + [n + str(k) for n in HOPS for k in range(N - 1)]
+
+
+def plan(topo, src, cores):
+    dsts = [c for c in cores if c != src]
+    off = [c for c in dsts if topo.chip(c) != topo.chip(src)]
+    on = [c for c in dsts if topo.chip(c) == topo.chip(src)]
+    out, used = {}, []
+    for grp in (off, on):
+        if not grp:
+            continue
+        free = [e for e in topo.engines(src, grp[0]) if e not in used]
+        w = 1
+        while 2 * w * len(grp) <= len(free):
+            w *= 2
+        for i, c in enumerate(grp):
+            out[c] = free[w * i:w * i + w]
+        used = used + [e for c in grp for e in out[c]]
+    return out
+
+
+def rank_program(g, core, T, topo):
+    rank = T.rank_of(core)
+    if rank is None:
+        return
+    cores = list(T.cores)
+    oth = [rank ^ (k + 1) for k in range(N - 1)]
+    eng = {"v": g.vector, "s": g.scalar, "t": g.tensor, "g": g, "y": g.sync}
+    cnt = {q: 0 for q in eng}
+    seen, writers, readers, dsum, pend, loc = {}, {}, {}, {}, {}, [0]
+    Qd = [slice(32 * q, 32 * q + 32) for q in range(4)]
+    lower, upper, every = slice(0, 64), slice(64, 128), slice(0, 128)
+    QM, q0 = Qd[rank], Qd[0]
+
+    def R(name, a=0, b=None, P=every, st=1):
+        return (name, P.start, P.stop, a, SCRATCH[name][1][1] if b is None else b, st)
+
+    def ind(win, off):
+        return ("ind", win, off)
+
+    def ap(x):
+        if x[0] == "ind":
+            return ap(x[1]).indirect(ap(x[2]))
+        if x[5] == 1:
+            return T[x[0]][x[1]:x[2], x[3]:x[4]]
+        return T[x[0]][x[1]:x[2], x[3]:x[4]:x[5]]
+
+    def flat(xs):
+        out = []
+        for x in xs:
+            if isinstance(x, tuple):
+                out += flat(x[1:]) if x[0] == "ind" else [x]
+        return out
+
+    def meet(x, y):
+        if x[1] >= y[2] or y[1] >= x[2] or x[3] >= y[4] or y[3] >= x[4]:
+            return False
+        return not (x[5] == y[5] and (x[3] - y[3]) % x[5])
+
+    def inside(x, y):
+        return y[1] <= x[1] and x[2] <= y[2] and y[3] <= x[3] and x[4] <= y[4] and (y[5] == 1 or y == x)
+
+    def wait(q, toks):
+        need = {}
+        for sem, val in toks:
+            if val > seen.get((q, sem), 0):
+                need[sem] = max(need.get(sem, 0), val)
+        for sem in need:
+            eng[q].wait_ge(T.sem[sem], need[sem])
+            seen[(q, sem)] = need[sem]
+
+    def deps(q, rs, ws):
+        toks = []
+        for x in rs + ws:
+            toks += [t for y, t in writers.get(x[0], []) if meet(x, y)]
+        for x in ws:
+            toks += [t for y, t in readers.get(x[0], []) if meet(x, y) and t[0] != q]
+        wait(q, toks)
+
+    def done(tok, rs, ws):
+        for x in rs:
+            readers.setdefault(x[0], []).append((x, tok))
+        for x in ws:
+            writers[x[0]] = [e for e in writers.get(x[0], []) if not inside(e[0], x)] + [(x, tok)]
+            readers[x[0]] = [e for e in readers.get(x[0], []) if not inside(e[0], x)]
+
+    def E(q, rs, ws, fn):
+        rs, ws = flat(rs), flat(ws)
+        deps(q, rs, ws)
+        fn(eng[q]).then_inc(T.sem[q], 1)
+        cnt[q] += 1
+        done((q, cnt[q]), rs, ws)
+
+    def D(q, out, in_, sem, fin=True, outap=None, inap=None):
+        rs, ws = flat([in_]), flat([out])
+        deps(q, rs, ws)
+        eng[q].dma_start(ap(out) if outap is None else outap, ap(in_) if inap is None else inap).then_inc(T.sem[sem], 16)
+        dsum[sem] = dsum.get(sem, 0) + 16
+        pend.setdefault(sem, []).append((rs, ws))
+        if fin:
+            for rs, ws in pend.pop(sem):
+                done((sem, dsum[sem]), rs, ws)
+
+    mine = plan(topo, core, cores)
+
+    def u8(v):
+        return v.bitcast(dt.uint8)
+
+    def u32(v):
+        return v.bitcast(dt.uint32)
+
+    land = {"ma": ("A1", 0, 12), "mp": ("AP", 0, 12), "qa": ("W1", X0, C), "sa": ("P1", X0, C), "mz": ("A2", 0, 12),
+            "qb": ("W1", X1, C), "sb": ("P1", X1, C), "qc": ("W2", X1, C), "sc": ("P2", X1, C)}
+
+    def landed(h, k):
+        n, a, w = land[h]
+        return R(n, a + w * k, a + w * k + w)
+
+    def send(h, src, codes=False):
+        deps("g", flat([src(k) for k in range(N - 1)]), [])
+        tr = []
+        for k, d in enumerate(oth):
+            rid, pid, _ = topo.addr(cores[d])
+            es = mine[cores[d]]
+            loc[0] += len(es)
+            s, t = ap(src(k)), ap(landed(h, k))
+            tr.append(RemoteDMATransfer(dst_ids=[DstId(rid=rid, pnc=pid)], dma_engine_mask=sum(1 << e for e in es),
+                                        remote_sem=T.sem[h + str(k)], srcs=[u8(s) if codes else s], dsts=[u8(t) if codes else t]))
+        g.remote_dma_fused(tr, local_sem=T.sem.loc)
+
+    def block(n):
+        return lambda k: R(n, C * k, C * k + C)
+
+    arrivals = []
+    for h in HOPS:
+        for k, d in enumerate(oth):
+            tok = (h + str(k), len(plan(topo, cores[d], cores)[core]))
+            arrivals.append(tok)
+            writers.setdefault(land[h][0], []).append((landed(h, k), tok))
+
+    def sc_(x):
+        return ap(x) if isinstance(x, tuple) else x
+
+    def ts(out, in0, s1, s2, o1, o2=None):
+        if o2 is None:
+            E("v", [in0, s1], [out], lambda e: e.tensor_scalar(ap(out), ap(in0), sc_(s1), None, o1))
+        else:
+            E("v", [in0, s1, s2], [out], lambda e: e.tensor_scalar(ap(out), ap(in0), sc_(s1), sc_(s2), o1, o2))
+
+    def tt(out, a, b, op):
+        E("v", [a, b], [out], lambda e: e.tensor_tensor(ap(out), ap(a), ap(b), op))
+
+    def cp(out, in_):
+        E("v", [in_], [out], lambda e: e.tensor_copy(ap(out), ap(in_)))
+
+    def scatter(win, off, val):
+        E("v", [off, val], [win], lambda e: e.tensor_copy(ap(win).indirect(ap(off)), ap(val)))
+
+    def fill(out, c):
+        E("v", [], [out], lambda e: e.memset(ap(out), c))
+
+    def scan(out, d0, d1):
+        E("v", [d0, d1], [out], lambda e: e.tensor_tensor_scan(ap(out), ap(d0), ap(d1), 0.0, A.mult, A.add))
+
+    def turn(out, in_):
+        E("v", [in_], [out], lambda e: e.transpose(ap(out), ap(in_)))
+
+    def ac(out, in_, scale=None, bias=None, fn=None):
+        f = fn or (AF.Copy if bias is None else AF.Identity)
+        kw = {}
+        if scale is not None:
+            kw["scale"] = sc_(scale)
+        if bias is not None:
+            kw["bias"] = sc_(bias)
+        E("s", [in_, scale, bias], [out], lambda e: e.activation(ap(out), ap(in_), f, **kw))
+
+    def co(out, c):
+        n = out[4] - out[3]
+        ac(out, R("j15" if n <= 192 else "ident", 0, n, slice(out[1], out[2])), scale=0.0, bias=c)
+
+    def iota(out, pattern, cm=0, flag=True):
+        if flag:
+            E("g", [], [out], lambda e: e.iota(ap(out), pattern, 0, cm, allow_small_or_imprecise_dtypes=True))
+        else:
+            E("g", [], [out], lambda e: e.iota(ap(out), pattern, 0, cm))
+
+    def pickq(out, win, off):
+        E("v", [win, off], [out], lambda e: e.tensor_copy(u32(ap(out)), u32(ap(win)).indirect(ap(off))))
+
+    def picks(out, win, off):
+        E("s", [win, off], [out], lambda e: e.activation(ap(out), ap(win).indirect(ap(off)), AF.Copy))
+
+    def quant(q, s, in_):
+        E("v", [in_], [q, s], lambda e: e.quantize_mx(ap(q), ap(s), ap(in_)))
+
+    def col(i, P=every):
+        return R("cf", i, i + 1, P)
+
+    def ends(name, P=every, n=12, a=0):
+        return R(name, a + 15, a + 16 * n, P, 16)
+
+    for i in range(2):
+        D("y", R("sb", 0, 12, slice(16 * i, 16 * i + 16)), None, "dst", False, inap=T.st[:])
+        D("s", R("sb", 12, 24, slice(16 * i, 16 * i + 16)), None, "dst", i == 1, inap=T.bt[:])
+    for i in range(2):
+        D("ys"[i], R("nxi", P=slice(16 * i, 16 * i + 16)), None, "dni", i == 1, inap=T.nx[:])
+    for i in range(16):
+        D("y", R("tba", P=slice(i, i + 1)), None, "dnx", False, inap=T.nx[:])
+        D("s", R("tba", P=slice(16 + i, 17 + i)), None, "dnx", i == 15, inap=T.nx[:])
+    for i in range(2, 8):
+        D("y", R("sb", 0, 12, slice(16 * i, 16 * i + 16)), None, "dsu", False, inap=T.st[:])
+        D("s", R("sb", 12, 24, slice(16 * i, 16 * i + 16)), None, "dsu", i == 7, inap=T.bt[:])
+    D("y", R("xs", 4 * Z0, 2 * X0), None, "dx", inap=T.x[:, 0:2 * X0 - 4 * Z0])
+    iota(R("pI"), [[1, 1]], 1, False)
+    iota(R("j15"), [[0, 12], [1, 16]])
+    iota(R("c16"), [[16, 12]])
+    iota(R("sg", 0, 36), [[0, 3], [1, 12]])
+    iota(R("sg", 36, 132), [[0, 3], [1, 32]])
+    iota(R("sg", 132, 141), [[0, 3], [1, 3]])
+    iota(R("sg", 141, 189), [[0, 12], [1, 4]])
+    iota(R("ident", 0, 256), [[1, 256]])
+    idn = R("ident")
+
+    r15, p31, qf, ev, od = [col(i) for i in range(5)]
+    off0, stu = R("lx", 0, 12), R("lx", 12, 24)
+    for P in (Qd[1], upper):
+        fill(R("tba", 0, 8, P), 0)
+    fill(off0, 0)
+    fill(R("M1"), 0)
+    fill(R("xs", 0, 4 * Z0), 0.0)
+    ts(R("ci", 0, 1), R("pI"), 15, None, A.bitwise_and)
+    ts(R("ci", 1, 2), R("pI"), 31, None, A.bitwise_and)
+    ts(R("ci", 2, 3), R("pI"), 5, None, A.arith_shift_right)
+    cp(R("cf", 0, 3), R("ci", 0, 3))
+    ts(R("mask"), R("j15"), r15, None, A.is_equal)
+    ts(R("mask2"), R("j15"), r15, 2.0, A.is_equal, A.mult)
+    ts(R("maskb"), R("j15", 0, 32), p31, None, A.is_gt)
+    ts(ev, p31, 16.0, None, A.is_lt)
+
+    sti = R("sb", 0, 12)
+    st0, bt0 = R("sb", 0, 12, q0), R("sb", 12, 24, q0)
+    la, lb, b2 = [R("l0", 12 * i, 12 * i + 12, q0) for i in range(3)]
+    fb, fc, fd, fe = [R("lf", 12 * i, 12 * i + 12, q0) for i in range(4)]
+    ts(la, st0, 3, None, A.arith_shift_right)
+    ts(lb, bt0, 1, None, A.bitwise_and)
+    ts(fb, st0, 2.0, None, A.mult)
+    ts(fc, la, -1023.0 / 64, None, A.mult)
+    tt(fd, fb, lb, A.add)
+    cp(R("nxf", P=q0), R("nxi", P=q0))
+    tt(fe, fd, fc, A.add)
+    turn(R("nxt", P=q0), R("nxf", P=q0))
+    ts(R("lx", 0, 12, q0), fe, 64.0, None, A.mult)
+
+    ac(R("seg"), R("j15"), fn=AF.Sign)
+    ac(R("sg", 0, 189), R("sg", 0, 189), fn=AF.Sign)
+    ac(R("i16"), R("c16", 0, 12), bias=r15)
+    for n in ("xa", "xb"):
+        ac(R(n, 3, 48, every, 4), R("i16"), bias=192.0)
+    for d in range(3):
+        ac(col(8 + d), r15, scale=191.0, bias=15.0 - 192 + C * d)
+    ac(R("ident", 256, 512), R("ident", 0, 256), bias=256.0)
+    ac(R("ident", 512, 1024), R("ident", 0, 512), bias=512.0)
+    ac(R("ident", 1024, 1104), R("ident", 0, 80), bias=1024.0)
+
+    tt(R("n1m"), ind(R("tba"), off0), R("mask2"), A.mult)
+    ts(b2, bt0, 1, None, A.arith_shift_right)
+    cp(stu, sti)
+    scan(R("n1s"), R("seg"), R("n1m"))
+    n1v = ends("n1s", q0)
+    cp(R("stf"), sti)
+    tt(R("E1", P=q0), n1v, b2, A.add)
+    for q in range(4):
+        ts(R("t1", P=Qd[q]), n1v, 1.0 / 1024, -255.5 / 512, A.mult, A.add)
+    cp(R("M1", P=QM), R("E1", P=q0))
+    send("ma", lambda k: R("M1"))
+    co(R("tb", 0, 4), 4096.0)
+    co(R("tb", 1028, 1032), 4096.0)
+    for i in range(8):
+        for h in range(2):
+            D("y", R("tb", 4 + 512 * h, 516 + 512 * h, slice(i, i + 1)), R("nxt", 32 * h, 32 * h + 16, q0), "dtr", i == 7 and h == 1)
+    D("y", R("xs", 2 * X0, 4 * X0), None, "dx1", inap=T.x[:, 2 * X0 - 4 * Z0:2048])
+    for i in range(1, 16):
+        D("y", R("tb", 4, 1028, slice(8 * i, 8 * i + 8)), R("tb", 4, 1028, slice(0, 8)), "dtq", i == 15)
+    D("y", R("ws", 0, 1024), None, "dw0", inap=T.w[:, 0:1024])
+
+    ac(R("val1"), ind(idn, stu), bias=float(Z0))
+    co(R("w1", 0, 192), 0.0)
+
+    def classes(t, eq, s, bb, bt, rr, pp, xx, kc, cross, fillers):
+        def part(name, j, n=12):
+            return R(name, n * j, n * j + n)
+
+        def gap():
+            if fillers:
+                fillers.pop(0)()
+        gap()
+        for j, d in enumerate(oth):
+            ts(part(eq, j), t, float(d), -16.0, A.is_equal, A.add)
+        gap()
+        scan(R(s), R("sg", 0, 36), R(eq, 0, 36))
+        ac(R(eq, 36, 72), R(eq, 0, 36), bias=16.0)
+        if cross:
+            for a, b, n, c, v in ((64, 32, 32, 2, 0), (32, 0, 32, 1, 0), (64, 0, 64, 0, 1), (96, 64, 32, 1, 1), (96, 0, 32, 2, 1)):
+                o, i_ = R("g9", c, 9, slice(a, a + n), 3), R(s, 11, 36, slice(b, b + n), 12)
+                if v:
+                    ts(o, i_, 0.5, None, A.mult)
+                else:
+                    ac(o, i_, scale=0.5)
+            gap()
+            scan(R("g9", 9, 18), R("sg", 132, 141), R("g9", 0, 9))
+        gap()
+        for j in range(3):
+            last = R(s, 12 * j + 11, 12 * j + 12)
+            before = R("g9", 11 + 3 * j, 12 + 3 * j) if cross else None
+            if j == 2 and cross:
+                ac(part(bb, j, 32), R("maskb"), scale=last, bias=before)
+            elif cross:
+                ts(part(bb, j, 32), R("maskb"), last, before, A.mult, A.add)
+            else:
+                ts(part(bb, j, 32), R("maskb"), last, None, A.mult)
+        gap()
+        turn(R(bt), R(bb))
+        gap()
+        scan(R(rr), R("sg", 36, 132), R(bt))
+        gap()
+        for j in range(3):
+            ts(part(pp, j), part(s, j), R(rr, 32 * j + 31, 32 * j + 32), col(kc + j), A.add, A.add)
+        gap()
+        for j in range(3):
+            tt(R(xx, j, 48, every, 4), part(pp, j), part(eq, 3 + j), A.mult)
+        gap()
+        scan(R(xx, 48, 96), R("sg", 141, 189), R(xx, 0, 48))
+        return R(xx, 51, 96, every, 4)
+
+    def own():
+        ts(R("off", P=QM), R("E1", P=q0), 4.0 - 1024 * rank, 1028.0, A.add, A.min)
+
+    def qx(i):
+        return lambda: quant(R("QX", 130 * i, 130 * i + 130), R("SX", 130 * i, 130 * i + 130), R("xs", 520 * i, 520 * i + 520))
+
+    def wq(i):
+        return lambda: quant(R("WQ", 128 * i, 128 * i + 128), R("WS", 128 * i, 128 * i + 128), R("ws", 512 * i, 512 * i + 512))
+
+    z1 = classes(R("t1"), "eqa", "sa", "ba", "bta", "ra", "pa", "xa", 8, False,
+                 [own, lambda: ts(R("maskc"), R("ident", 0, 32), p31, None, A.is_gt), lambda: None] + [qx(i) for i in range(4)])
+    slot1 = R("sl", 0, 12)
+    cp(slot1, z1)
+    ac(R("MP"), z1)
+    send("mp", lambda k: R("MP"))
+    ac(od, ev, scale=-1.0, bias=1.0)
+    ac(col(6), ev, scale=float(Z0))
+    ac(col(7), qf, scale=524288.0)
+    ac(col(15), col(7), scale=od)
+    for d in range(3):
+        ac(col(11 + d), qf, scale=3072.0, bias=col(8 + d))
+    ac(R("park"), R("i16"), bias=288.0)
+    ac(R("K2"), R("i16"), scale=od, bias=col(6))
+    co(R("g9", 0, 9), 0.0)
+    ac(R("L0f", P=QM), R("stf", P=QM), bias=float(Z0))
+    co(R("w2", 0, 192), 0.0)
+
+    scatter(R("w1"), slot1, R("val1"))
+    tt(R("f1", 0, 192), R("w1", 0, 192), R("mask"), A.mult)
+    for k, d in enumerate(oth):
+        ts(R("off", P=Qd[d]), R("A1", 12 * k, 12 * k + 12, Qd[d]), 4.0 - 1024 * rank, 1028.0, A.add, A.min)
+    scan(R("f1", 192, 384), R("seg"), R("f1", 0, 192))
+    ts(R("c1i"), R("off"), 0.5, Z0 - 2.25, A.mult, A.add)
+    cp(R("stl"), ends("f1", a=192))
+    tt(R("n2m"), ind(R("tb"), R("off")), R("mask"), A.mult)
+    pickq(R("Q1"), R("QX"), R("stl"))
+    picks(R("S1"), R("SX"), R("stl"))
+    D("s", R("ws", 1024, 3072), None, "dw1", inap=T.w[:, 1024:3072])
+    send("qa", block("Q1"), True)
+    send("sa", block("S1"))
+    D("y", R("W1", 0, X0), R("QX"), "dq1", False, outap=u8(ap(R("W1", 0, X0))), inap=u8(ap(R("QX"))))
+    D("y", R("P1", 0, X0), R("SX"), "dq1")
+    D("y", R("W2", 0, X1), R("W1", 0, X1), "dq2", False, outap=u8(ap(R("W2", 0, X1))), inap=u8(ap(R("W1", 0, X1))))
+    D("y", R("P2", 0, X1), R("P1", 0, X1), "dq2")
+    scan(R("n2s"), R("seg"), R("n2m"))
+    cp(R("c1u"), R("c1i"))
+    n2v = ends("n2s")
+    ts(R("t2"), n2v, 1.0 / 512, -255.5 / 512, A.mult, A.add)
+    ac(R("uf1"), ind(idn, R("c1u")), scale=2048.0)
+    ac(R("n2k"), n2v, scale=2048.0, bias=float(X1))
+    z2 = classes(R("t2"), "eqb", "sc", "bb", "btb", "rb", "pb", "xb", 11, True,
+                 [lambda: ts(R("c1o"), R("c1i"), od, float(-X1), A.mult, A.add), wq(0), wq(1)])
+    for k, d in enumerate(oth):
+        ac(R("L0f", P=Qd[d]), R("AP", 12 * k, 12 * k + 12, Qd[d]), bias=float(X0))
+    ac(R("L0e"), R("L0f"), scale=ev)
+    tt(R("M2"), R("n2k"), z2, A.add)
+    send("mz", lambda k: R("M2"))
+    slot2 = R("sl", 12, 24)
+    cp(slot2, z2)
+    cp(R("L0u"), R("L0f"))
+    tt(R("val2"), ind(idn, R("L0u")), R("uf1"), A.add)
+    wq(2)()
+    scatter(R("w2"), slot2, R("val2"))
+    tt(R("SBm"), R("L0e"), R("c1o"), A.add)
+    co(R("pw", 0, 288), 0.0)
+    co(R("PZ"), 0.0)
+    co(R("g3", 0, 3), 0.0)
+    co(R("F32"), 0.0)
+    near, far0, far1 = sorted(range(N - 1), key=lambda k: topo.chip(cores[oth[k]]) != topo.chip(core))
+    tc = [R("tc", 32 * i, 32 * i + 32) for i in range(7)]
+
+    def s0():
+        tt(R("f2", 0, 192), R("w2", 0, 192), R("mask"), A.mult)
+
+    def e0():
+        tt(R("Zf", 0, 12), R("n2k"), R("SBm"), A.add)
+
+    def s1():
+        scan(R("f2", 192, 384), R("seg"), R("f2", 0, 192))
+        wq(3)()
+
+    def e1():
+        tt(R("Zf", 12, 24), R("Zf", 0, 12), landed("mz", near), A.min)
+
+    def s2():
+        for q in (1, 3, 0, 2):
+            (ac if q % 2 else cp)(R("hg", 0, 12, Qd[q]), ends("f2", Qd[q ^ 1], a=192))
+
+    def e2():
+        tt(R("Zf", 24, 36), landed("mz", far0), landed("mz", far1), A.min)
+
+    def s3():
+        tt(R("hg", 12, 24), ends("f2", a=192), R("hg", 0, 12), A.add)
+
+    def e3():
+        tt(R("Zi", 0, 12), R("Zf", 24, 36), R("Zf", 12, 24), A.min)
+
+    def s4():
+        ac(R("hg", 24, 36, upper), R("hg", 12, 24, lower))
+        cp(R("hg", 24, 36, lower), R("hg", 12, 24, upper))
+
+    def e4():
+        ts(R("Zi", 12, 24), R("Zi", 0, 12), 20, None, A.arith_shift_right)
+        ts(R("Zi", 24, 36), R("Zi", 0, 12), 11, 511, A.arith_shift_right, A.bitwise_and)
+        ts(R("Zi", 36, 48), R("Zi", 0, 12), 2047, None, A.bitwise_and)
+
+    def s5():
+        tt(R("fa", 0, 12), R("hg", 12, 24), R("hg", 24, 36), A.add)
+
+    def e5():
+        ts(R("PZ", 0, 12), R("Zi", 12, 24), float(rank), None, A.is_equal)
+        ac(R("pr"), R("PZ", 0, 12), scale=-1024.0)
+        ts(R("ze", 0, 12), R("Zi", 24, 36), ev, None, A.mult)
+
+    def s6():
+        ts(R("l34", 0, 12), R("fa", 0, 12), 1.0 / 2048, None, A.mult)
+        ts(R("fa", 24, 36), R("fa", 0, 12), 2047, None, A.bitwise_and)
+
+    def e6():
+        turn(tc[0], R("PZ"))
+        tt(R("ze", 12, 24), R("ze", 0, 12), R("K2"), A.add)
+
+    def s7():
+        cp(R("l34", 12, 24), R("fa", 24, 36))
+
+    def e7():
+        scan(tc[1], R("seg", 0, 32), tc[0])
+        cp(R("zl", 12, 24), R("ze", 12, 24))
+
+    def s8():
+        pickq(R("Q3"), R("QX"), R("l34", 0, 12))
+        picks(R("S3"), R("SX"), R("l34", 0, 12))
+        send("qb", block("Q3"), True)
+
+    def e8():
+        for a, b, n, c, v in ((32, 0, 32, 1, 0), (64, 32, 32, 2, 0), (64, 0, 64, 0, 1), (96, 64, 32, 1, 1), (96, 0, 32, 2, 1)):
+            (cp if v else ac)(R("g3", c, c + 1, slice(a, a + n)), R("tc", 47, 48, slice(b, b + n)))
+        tt(R("pz", 0, 12), R("park"), R("pr"), A.add)
+
+    def e9():
+        scan(R("g3", 3, 6), R("sg", 132, 135), R("g3", 0, 3))
+        ac(R("uf2"), ind(idn, R("zl", 12, 24)), scale=2048.0, bias=col(15))
+
+    def s9():
+        pickq(R("Q4"), R("W1", 0, X1), R("l34", 12, 24))
+        picks(R("S4"), R("P1", 0, X1), R("l34", 12, 24))
+        send("sb", block("S3"))
+        send("qc", block("Q4"), True)
+        send("sc", block("S4"))
+
+    for fn in (s0, e0, s1, s2, e1, s3, e2, s4, e3, s5, e4, s6, e5, s7, e6, s8, e7, e8, e9, s9):
+        fn()
+    cp(R("zl", 0, 12), R("Zi", 36, 48))
+    ts(tc[2], R("maskc"), R("tc", 47, 48), R("g3", 5, 6), A.mult, A.add)
+    turn(tc[3], tc[2])
+    wq(4)()
+    scan(tc[4], R("sg", 36, 68), tc[3])
+    wq(5)()
+    ts(tc[5], tc[1], R("tc", 159, 160), -1.0, A.add, A.add)
+    turn(tc[6], tc[5])
+    tt(R("val3"), ind(idn, R("zl", 0, 12)), R("uf2"), A.add)
+    tt(R("pz", 12, 24), R("tc", 192, 204), R("pz", 0, 12), A.max)
+    slot3 = R("sl", 24, 36)
+    cp(slot3, R("pz", 12, 24))
+    scatter(R("pw"), slot3, R("val3"))
+    turn(R("f3"), R("pw", 0, 288))
+    for q in (1, 3, 0, 2):
+        (ac if q % 2 else cp)(R("hm", P=Qd[q]), R("f3", 0, 288, Qd[q ^ 1], 16))
+    for k in range(2):
+        tt(R("F32", 16 * k, 16 * k + 9), R("f3", 16 * k, 288, every, 32), R("hm", k, 18, every, 2), A.add)
+    turn(R("TF"), R("F32"))
+    ac(R("hx", P=upper), R("TF", P=lower))
+    cp(R("hx", P=lower), R("TF", P=upper))
+    for i in range(4):
+        h = i // 2
+        tt(R("DD", 16 * i, 16 * i + 16), R("TF", h, 32, every, 2), R("hx", h, 32, every, 2), A.add)
+    turn(R("LT"), R("DD"))
+    tt(R("SS"), R("TF"), R("hx"), A.add)
+    ts(R("HU"), R("LT"), 1.0 / 2048, None, A.mult)
+    ts(R("li"), R("LT"), 2047, None, A.bitwise_and)
+    ts(R("idi", 0, 32), R("SS"), 19, None, A.arith_shift_right)
+    ts(R("idi", 32, 64), R("SS"), 11, 255, A.arith_shift_right, A.bitwise_and)
+    ts(R("idi", 64, 96), R("SS"), 1.0, -1.0, A.is_ge, A.add)
+
+    def products(i, q, s, h):
+        for o in range(O):
+            c, d = 128 * ((2 - i) * O + o), 512 * (2 * o + h)
+            a, b = L * h, L * h + L
+            E("t", [R(q, a, b), R(s, a, b), R("WQ", c, c + 128), R("WS", c, c + 128)], [R("ps", d, d + L)] if i == 2 else [],
+              lambda e: e.matmul_mx(ap(R("ps", d, d + L)), ap(R("WQ", c, c + 128)), ap(R("WS", c, c + 128)), ap(R(q, a, b)), ap(R(s, a, b)), i == 0, i == 2))
+
+    for i, (q, s, w, p, l, a) in enumerate((("G2", "H2", R("QX"), R("SX"), "HU", 0), ("G1", "H1", R("W1"), R("P1"), "LU", 16), ("G0", "H0", R("W2"), R("P2"), "LU", 0))):
+        for h in range(2):
+            lst = R(l, 32 * h + a, 32 * h + a + 9)
+            pickq(R(q, L * h, L * h + L), w, lst)
+            picks(R(s, L * h, L * h + L), p, lst)
+            products(i, q, s, h)
+            if i == 0 and h == 0:
+                cp(R("LU"), R("li"))
+    tt(R("idt", 0, 32), R("idi", 0, 32), R("idi", 64, 96), A.add)
+    tt(R("idt", 32, 64), R("idi", 32, 64), R("idi", 64, 96), A.add)
+    for h in range(2):
+        cp(R("ysb", h, M, every, 2), R("ps", 512 * h, 512 * h + L))
+        ac(R("ysb", M + h, 2 * M, every, 2), R("ps", 1024 + 512 * h, 1024 + 512 * h + L))
+    for o in range(2):
+        D("y", None, R("idt", 32 * o, 32 * o + 32, slice(16, 25)), "di%d" % o, outap=T.id[o:o + 1, :])
+    D("y", None, R("ysb", 0, M), "dy0", outap=T.y[:, 0:M])
+    D("s", None, R("ysb", M, 2 * M), "dy1", outap=T.y[:, M:2 * M])
+
+    wait("g", [(q, cnt[q]) for q in ("v", "s", "t", "g")] + [("loc", loc[0])] + [(s, dsum[s]) for s in DMAS] + arrivals)

@@ -3,10 +3,11 @@ from concourse.mybir import dt, AluOpType as A, ActivationFunctionType as AF
 
 N, V, M, O = 4, 192, 288, 2
 C = 64
-Z0 = 8
-X0 = Z0 + 512
-X1 = X0 + 192
-L = M // 2
+ZC = 192
+XO = 200
+X1 = XO + 512
+R0 = 123
+PARTS = ((0, 160), (160, 288))
 F, I, U, B = "float32", "int32", "uint16", "bfloat16"
 Q8, S8 = "float8_e4m3fn_x4", "uint8"
 
@@ -16,31 +17,31 @@ def _sb(w, d):
 
 
 SCRATCH = {
-    "tba": _sb(1024, I), "tb": _sb(1032, F), "sb": _sb(24, I), "nxi": _sb(64, I), "nxf": _sb(64, F), "nxt": _sb(64, F),
-    "xs": _sb(4 * X0, B), "ws": _sb(3072, B),
-    "QX": _sb(X0, Q8), "SX": _sb(X0, S8), "W1": _sb(X1 + 192, Q8), "P1": _sb(X1 + 192, S8), "W2": _sb(X1 + 192, Q8), "P2": _sb(X1 + 192, S8),
+    "tba": _sb(1024, I), "tab": _sb(4096, F), "land": ("dram", [4, 128, 16], F), "sb": _sb(32, I), "nxi": _sb(32, I), "nxf": _sb(32, F), "nxt": _sb(32, F),
+    "xs": _sb(4 * 520, B), "ws": _sb(3072, B),
+    "QX": _sb(X1, Q8), "SX": _sb(X1, S8), "W1": _sb(X1 + 192, Q8), "P1": _sb(X1 + 192, S8), "W2": _sb(X1 + 192, Q8), "P2": _sb(X1 + 192, S8),
     "WQ": _sb(768, Q8), "WS": _sb(768, S8),
     "Q1": _sb(192, Q8), "S1": _sb(192, S8), "Q3": _sb(192, Q8), "S3": _sb(192, S8), "Q4": _sb(192, Q8), "S4": _sb(192, S8),
     "G0": _sb(288, Q8), "H0": _sb(288, S8), "G1": _sb(288, Q8), "H1": _sb(288, S8), "G2": _sb(288, Q8), "H2": _sb(288, S8),
-    "j15": _sb(192, F), "pI": _sb(1, I), "c16": _sb(12, F), "ident": _sb(1104, F), "mask": _sb(192, F), "mask2": _sb(192, F), "seg": _sb(192, F), "maskb": _sb(32, F),
-    "maskc": _sb(32, F), "sg": _sb(192, F), "ci": _sb(4, I), "cf": _sb(24, F), "i16": _sb(12, F), "park": _sb(12, F), "K2": _sb(12, F),
-    "l0": _sb(36, I), "lf": _sb(48, F), "lx": _sb(24, U), "stf": _sb(12, F),
-    "val1": _sb(192, F), "n1m": _sb(192, F), "n1s": _sb(192, F), "t1": _sb(12, I), "E1": _sb(12, F), "M1": _sb(12, U), "A1": _sb(36, U),
-    "MP": _sb(12, B), "AP": _sb(36, B),
-    "eqa": _sb(72, F), "sa": _sb(36, F), "ba": _sb(96, F), "bta": _sb(96, F), "ra": _sb(96, F), "pa": _sb(36, F), "xa": _sb(96, F),
-    "eqb": _sb(72, F), "sc": _sb(36, F), "bb": _sb(96, F), "btb": _sb(96, F), "rb": _sb(96, F), "pb": _sb(36, F), "xb": _sb(96, F), "g9": _sb(18, F),
-    "sl": _sb(36, U), "w1": _sb(384, F), "w2": _sb(384, F), "pw": _sb(480, F), "f1": _sb(384, F), "f2": _sb(384, F), "f3": _sb(288, F),
-    "stl": _sb(12, U), "off": _sb(12, U), "n2m": _sb(192, F), "n2s": _sb(192, F), "t2": _sb(12, I), "c1i": _sb(12, I), "c1u": _sb(12, U), "c1o": _sb(12, F),
-    "L0f": _sb(12, F), "L0e": _sb(12, F), "L0u": _sb(12, U), "SBm": _sb(12, F), "n2k": _sb(12, F), "M2": _sb(12, F), "A2": _sb(36, F), "uf1": _sb(192, F), "val2": _sb(192, F),
-    "hg": _sb(36, F), "fa": _sb(48, I), "l34": _sb(24, U),
-    "Zf": _sb(36, F), "Zi": _sb(48, I), "zl": _sb(24, U), "ze": _sb(24, F), "uf2": _sb(192, F), "val3": _sb(192, F), "pr": _sb(12, F), "PZ": _sb(32, F),
-    "tc": _sb(224, F), "g3": _sb(6, F), "pz": _sb(24, F), "hm": _sb(18, F), "F32": _sb(32, F), "TF": _sb(32, F), "hx": _sb(32, F), "DD": _sb(64, I), "LT": _sb(64, I),
-    "SS": _sb(32, I), "li": _sb(64, I), "LU": _sb(64, U), "HU": _sb(64, U), "idi": _sb(96, I), "idt": _sb(64, F), "ysb": _sb(576, F),
+    "pI": _sb(2, I), "ci": _sb(8, I), "cf": _sb(32, F), "ident": _sb(X1, F), "identC": _sb(512, F), "identR": _sb(200, F),
+    "seg32": _sb(192, F), "one": _sb(192, B), "K": _sb(192, F), "cl": _sb(32, F), "cu": _sb(16, U),
+    "l0": _sb(36, I), "lf": _sb(48, F), "la": _sb(12, U), "b2": _sb(6, I),
+    "GA": _sb(192, I), "GT": _sb(192, I), "eqa": _sb(192, F), "cua": _sb(192, F), "za": _sb(192, F), "zt": _sb(192, F), "zs": _sb(192, F),
+    "E1": _sb(6, F), "M1": _sb(12, U), "A1": _sb(36, U), "LM": _sb(12, U), "val1": _sb(96, F), "w1": _sb(384, F), "wt": _sb(192, F),
+    "Fa": _sb(32, F), "Ta": _sb(32, F), "Za": _sb(64, F), "La": _sb(64, F), "stl": _sb(12, U),
+    "GB": _sb(96, I), "PT": _sb(96, I), "kw": _sb(16, I), "c2": _sb(6, I), "c2u": _sb(6, U), "vi": _sb(12, I), "vf": _sb(12, F),
+    "XV": _sb(96, F), "V0": _sb(96, F), "V1": _sb(96, F), "val": _sb(96, F),
+    "X": _sb(192, B), "XT": _sb(192, B), "cb": _sb(192, B), "g3": _sb(8, F), "cub": _sb(192, F), "zu": _sb(192, F), "zv": _sb(192, F),
+    "sl": _sb(12, U), "pw": _sb(1280, F), "T1": _sb(480, F),
+    "Fs": _sb(32, F), "Hs": _sb(32, F), "Gs": _sb(32, F), "Ts": _sb(32, F), "Us": _sb(32, F), "Ss": _sb(32, F), "Zs": _sb(64, F), "Ls": _sb(64, F), "ls": _sb(24, U),
+    "Fp": _sb(64, F), "Hp": _sb(64, F), "Gp": _sb(64, F), "Tp": _sb(64, F), "Up": _sb(64, F), "Sp": _sb(64, F), "Zp": _sb(64, F), "Lp": _sb(64, F), "lp": _sb(54, U),
+    "idt": _sb(32, F), "ysb": _sb(576, F),
     "ps": ("psum", [128, 2048], F),
 }
-DMAS = ["dnx", "dst", "dsu", "dx", "dx1", "dw0", "dw1", "dni", "dtr", "dtq", "dq1", "dq2", "dy0", "dy1", "di0", "di1"]
-HOPS = ("ma", "mp", "qa", "sa", "mz", "qb", "sb", "qc", "sc")
-SEMAPHORES = ["v", "s", "t", "g", "loc"] + DMAS + [n + str(k) for n in HOPS for k in range(N - 1)]
+DMAS = ["dnx", "dst", "dx", "dx1", "dw0", "dw1", "dw2", "dni", "dto", "dtr", "dq1", "dq2", "dq3", "dy0", "dy1", "di0", "di1"]
+HOPS = ("nt", "ma", "qa", "sa", "qb", "qc", "sb", "sc")
+CALLS = ("nt", "ma", "qa", "sa", "qb", "qc", "sb")
+SEMAPHORES = ["v", "s", "t", "g"] + DMAS + [n + str(k) for n in HOPS for k in range(N - 1)] + ["l" + n for n in CALLS]
 
 
 def plan(topo, src, cores):
@@ -66,13 +67,14 @@ def rank_program(g, core, T, topo):
     if rank is None:
         return
     cores = list(T.cores)
-    oth = [rank ^ (k + 1) for k in range(N - 1)]
+    to = [(rank + 1 + k) % N for k in range(N - 1)]
+    frm = [(rank - 1 - k) % N for k in range(N - 1)]
     eng = {"v": g.vector, "s": g.scalar, "t": g.tensor, "g": g, "y": g.sync}
     cnt = {q: 0 for q in eng}
-    seen, writers, readers, dsum, pend, loc = {}, {}, {}, {}, {}, [0]
+    seen, writers, readers, dsum, pend, left = {}, {}, {}, {}, {}, {}
     Qd = [slice(32 * q, 32 * q + 32) for q in range(4)]
     lower, upper, every = slice(0, 64), slice(64, 128), slice(0, 128)
-    QM, q0 = Qd[rank], Qd[0]
+    QM, q3 = Qd[rank], Qd[3]
 
     def R(name, a=0, b=None, P=every, st=1):
         return (name, P.start, P.stop, a, SCRATCH[name][1][1] if b is None else b, st)
@@ -83,6 +85,8 @@ def rank_program(g, core, T, topo):
     def ap(x):
         if x[0] == "ind":
             return ap(x[1]).indirect(ap(x[2]))
+        if x[0] == "land":
+            return T.land[x[3]]
         if x[5] == 1:
             return T[x[0]][x[1]:x[2], x[3]:x[4]]
         return T[x[0]][x[1]:x[2], x[3]:x[4]:x[5]]
@@ -143,42 +147,48 @@ def rank_program(g, core, T, topo):
             for rs, ws in pend.pop(sem):
                 done((sem, dsum[sem]), rs, ws)
 
-    mine = plan(topo, core, cores)
-
     def u8(v):
         return v.bitcast(dt.uint8)
 
     def u32(v):
         return v.bitcast(dt.uint32)
 
-    land = {"ma": ("A1", 0, 12), "mp": ("AP", 0, 12), "qa": ("W1", X0, C), "sa": ("P1", X0, C), "mz": ("A2", 0, 12),
-            "qb": ("W1", X1, C), "sb": ("P1", X1, C), "qc": ("W2", X1, C), "sc": ("P2", X1, C)}
+    land = {"ma": ("A1", 0, 12), "qa": ("W1", 0, C), "sa": ("P1", 0, C), "qb": ("W1", X1, C), "sb": ("P1", X1, C), "qc": ("W2", X1, C), "sc": ("P2", X1, C)}
 
-    def landed(h, k):
+    def landed(h, k, sender):
+        if h == "nt":
+            return R("land", sender, sender + 1)
         n, a, w = land[h]
         return R(n, a + w * k, a + w * k + w)
 
-    def send(h, src, codes=False):
-        deps("g", flat([src(k) for k in range(N - 1)]), [])
-        tr = []
-        for k, d in enumerate(oth):
-            rid, pid, _ = topo.addr(cores[d])
-            es = mine[cores[d]]
-            loc[0] += len(es)
-            s, t = ap(src(k)), ap(landed(h, k))
-            tr.append(RemoteDMATransfer(dst_ids=[DstId(rid=rid, pnc=pid)], dma_engine_mask=sum(1 << e for e in es),
-                                        remote_sem=T.sem[h + str(k)], srcs=[u8(s) if codes else s], dsts=[u8(t) if codes else t]))
-        g.remote_dma_fused(tr, local_sem=T.sem.loc)
+    def share(src, dst, h):
+        es = plan(topo, src, cores)[dst]
+        return es[:len(es) // 2] if h == "sb" else es[len(es) // 2:] if h == "sc" else es
+
+    def send(*parts, codes=False):
+        deps("g", flat([src(k) for h, src in parts for k in range(N - 1)]), [])
+        tr, n = [], 0
+        for h, src in parts:
+            for k, d in enumerate(to):
+                rid, pid, _ = topo.addr(cores[d])
+                es = share(core, cores[d], h)
+                n += len(es)
+                s, t = ap(src(k)), ap(landed(h, k, rank))
+                tr.append(RemoteDMATransfer(dst_ids=[DstId(rid=rid, pnc=pid)], dma_engine_mask=sum(1 << e for e in es),
+                                            remote_sem=T.sem[h + str(k)], srcs=[u8(s) if codes else s], dsts=[u8(t) if codes else t]))
+        left[parts[0][0]] = ("l" + parts[0][0], n)
+        g.remote_dma_fused(tr, local_sem=T.sem["l" + parts[0][0]])
 
     def block(n):
         return lambda k: R(n, C * k, C * k + C)
 
     arrivals = []
     for h in HOPS:
-        for k, d in enumerate(oth):
-            tok = (h + str(k), len(plan(topo, cores[d], cores)[core]))
+        for k, d in enumerate(frm):
+            tok = (h + str(k), len(share(cores[d], core, h)))
             arrivals.append(tok)
-            writers.setdefault(land[h][0], []).append((landed(h, k), tok))
+            x = landed(h, k, d)
+            writers.setdefault(x[0], []).append((x, tok))
 
     def sc_(x):
         return ap(x) if isinstance(x, tuple) else x
@@ -201,8 +211,8 @@ def rank_program(g, core, T, topo):
     def fill(out, c):
         E("v", [], [out], lambda e: e.memset(ap(out), c))
 
-    def scan(out, d0, d1):
-        E("v", [d0, d1], [out], lambda e: e.tensor_tensor_scan(ap(out), ap(d0), ap(d1), 0.0, A.mult, A.add))
+    def scan(out, d0, d1, init=0.0, o0=A.mult, o1=A.add):
+        E("v", [d0, d1, init], [out], lambda e: e.tensor_tensor_scan(ap(out), ap(d0), ap(d1), sc_(init), o0, o1))
 
     def turn(out, in_):
         E("v", [in_], [out], lambda e: e.transpose(ap(out), ap(in_)))
@@ -216,9 +226,11 @@ def rank_program(g, core, T, topo):
             kw["bias"] = sc_(bias)
         E("s", [in_, scale, bias], [out], lambda e: e.activation(ap(out), ap(in_), f, **kw))
 
+    def idn(n, P=every):
+        return R("ident", XO, XO + n, P)
+
     def co(out, c):
-        n = out[4] - out[3]
-        ac(out, R("j15" if n <= 192 else "ident", 0, n, slice(out[1], out[2])), scale=0.0, bias=c)
+        ac(out, idn(min(256, len(range(out[3], out[4], out[5]))), slice(out[1], out[2])), scale=0.0, bias=c)
 
     def iota(out, pattern, cm=0, flag=True):
         if flag:
@@ -238,349 +250,272 @@ def rank_program(g, core, T, topo):
     def col(i, P=every):
         return R("cf", i, i + 1, P)
 
-    def ends(name, P=every, n=12, a=0):
-        return R(name, a + 15, a + 16 * n, P, 16)
+    def qx(i):
+        a = ZC + 130 * i
+        quant(R("QX", a, a + 130), R("SX", a, a + 130), R("xs", 520 * i, 520 * i + 520))
 
-    for i in range(2):
-        D("y", R("sb", 0, 12, slice(16 * i, 16 * i + 16)), None, "dst", False, inap=T.st[:])
-        D("s", R("sb", 12, 24, slice(16 * i, 16 * i + 16)), None, "dst", i == 1, inap=T.bt[:])
-    for i in range(2):
-        D("ys"[i], R("nxi", P=slice(16 * i, 16 * i + 16)), None, "dni", i == 1, inap=T.nx[:])
-    for i in range(16):
-        D("y", R("tba", P=slice(i, i + 1)), None, "dnx", False, inap=T.nx[:])
-        D("s", R("tba", P=slice(16 + i, 17 + i)), None, "dnx", i == 15, inap=T.nx[:])
-    for i in range(2, 8):
-        D("y", R("sb", 0, 12, slice(16 * i, 16 * i + 16)), None, "dsu", False, inap=T.st[:])
-        D("s", R("sb", 12, 24, slice(16 * i, 16 * i + 16)), None, "dsu", i == 7, inap=T.bt[:])
-    D("y", R("xs", 4 * Z0, 2 * X0), None, "dx", inap=T.x[:, 0:2 * X0 - 4 * Z0])
-    iota(R("pI"), [[1, 1]], 1, False)
-    iota(R("j15"), [[0, 12], [1, 16]])
-    iota(R("c16"), [[16, 12]])
-    iota(R("sg", 0, 36), [[0, 3], [1, 12]])
-    iota(R("sg", 36, 132), [[0, 3], [1, 32]])
-    iota(R("sg", 132, 141), [[0, 3], [1, 3]])
-    iota(R("sg", 141, 189), [[0, 12], [1, 4]])
-    iota(R("ident", 0, 256), [[1, 256]])
-    idn = R("ident")
+    def wq(i):
+        quant(R("WQ", 128 * i, 128 * i + 128), R("WS", 128 * i, 128 * i + 128), R("ws", 512 * i, 512 * i + 512))
 
-    r15, p31, qf, ev, od = [col(i) for i in range(5)]
-    off0, stu = R("lx", 0, 12), R("lx", 12, 24)
-    for P in (Qd[1], upper):
-        fill(R("tba", 0, 8, P), 0)
-    fill(off0, 0)
-    fill(R("M1"), 0)
-    fill(R("xs", 0, 4 * Z0), 0.0)
-    ts(R("ci", 0, 1), R("pI"), 15, None, A.bitwise_and)
-    ts(R("ci", 1, 2), R("pI"), 31, None, A.bitwise_and)
-    ts(R("ci", 2, 3), R("pI"), 5, None, A.arith_shift_right)
-    cp(R("cf", 0, 3), R("ci", 0, 3))
-    ts(R("mask"), R("j15"), r15, None, A.is_equal)
-    ts(R("mask2"), R("j15"), r15, 2.0, A.is_equal, A.mult)
-    ts(R("maskb"), R("j15", 0, 32), p31, None, A.is_gt)
-    ts(ev, p31, 16.0, None, A.is_lt)
+    def copy(w, p, a, b, q, s, sem):
+        D("y", R(w, a, b), R(q, a, b), sem, False, outap=u8(ap(R(w, a, b))), inap=u8(ap(R(q, a, b))))
+        D("y", R(p, a, b), R(s, a, b), sem)
 
-    sti = R("sb", 0, 12)
-    st0, bt0 = R("sb", 0, 12, q0), R("sb", 12, 24, q0)
-    la, lb, b2 = [R("l0", 12 * i, 12 * i + 12, q0) for i in range(3)]
-    fb, fc, fd, fe = [R("lf", 12 * i, 12 * i + 12, q0) for i in range(4)]
+    g6, g7 = slice(96, 112), slice(112, 128)
+    fill(R("sb", P=q3), 0)
+    fill(R("nxf"), 0.0)
+    for h in range(2):
+        D("ys"[h], R("nxi", P=slice(32 * h, 32 * h + 16)), None, "dni", h == 1, inap=T.nx[:, 32 * h:32 * h + 32])
+    for i, t in enumerate((T.st, T.bt)):
+        D("ys"[i], R("sb", 16 * i, 16 * i + 12, g7), None, "dst", False, inap=t[:])
+        D("ys"[i], R("sb", 16 * i + 2, 16 * i + 14, g6), None, "dst", i == 1, inap=t[:])
+    for p in range(R0, 128):
+        D("ys"[p % 2], R("tba", P=slice(p, p + 1)), None, "dnx", p == 127, inap=T.nx[:])
+    D("y", R("xs", 32, 1040), None, "dx", inap=T.x[:, 0:1008])
+    D("y", R("xs", 1040, 2080), None, "dx1", inap=T.x[:, 1008:2048])
+    D("y", R("ws", 0, 1024), None, "dw0", inap=T.w[:, 0:1024])
+    iota(R("pI"), [[128 - R0 + 1 + rank, 2]], 1, False)
+    iota(idn(256), [[1, 256]])
+    iota(R("tab", 0, 384), [[0, 384]])
+
+    pi = R("pI", 0, 1)
+    r15, p31, qf, pf, e127, s1, s2, basea, da = col(0), col(1), col(2), col(4), col(5), col(6), col(7), col(8), col(9)
+    fill(R("la"), 0)
+    fill(R("LM"), XO)
+    ts(R("ci", 0, 1), pi, 15, None, A.bitwise_and)
+    ts(R("ci", 1, 2), pi, 31, None, A.bitwise_and)
+    ts(R("ci", 2, 3), pi, 5, None, A.arith_shift_right)
+    ts(R("ci", 3, 4), R("pI", 1, 2), 3, None, A.bitwise_and)
+    ts(e127, pi, 127.0, None, A.is_equal)
+    cp(pf, pi)
+    cp(R("cf", 0, 4), R("ci", 0, 4))
+    fill(R("tba", 0, 384, slice(0, R0)), 4096)
+    ts(col(10), r15, 5.0, 6.0, A.is_equal, A.mult)
+    ts(col(13), r15, 0.0, None, A.is_equal)
+    ts(col(11), r15, 2.0, None, A.is_lt)
+    ts(col(12), r15, 2.0, None, A.is_equal)
+    ts(col(14), p31, 16.0, 32.0, A.is_ge, A.mult)
+    for h in range(2):
+        P = slice(32 * h, 32 * h + 16)
+        ts(R("nxf", P=P), R("nxi", P=P), 2048.0 * rank, None, A.add)
+    fill(R("tba", 384, 512, slice(0, R0)), 4096)
+    turn(R("nxt"), R("nxf"))
+    fill(R("tba", 512, 768, slice(0, R0)), 4096)
+    send(("nt", lambda k: R("nxt", 0, 16)))
+    iota(R("tab", 384, 896), [[0, 512]])
+    junk = [lambda a=a: co(R("tab", a, min(a + 256, 4096)), 0.0) for a in range(896, 4096, 256)]
+
+    def some(n):
+        for i in range(min(n, len(junk))):
+            junk.pop(0)()
+    ac(s1, e127, scale=2.0 - 1.0 / 512, bias=1.0 / 512)
+    ac(s2, e127, scale=255.5 / 512, bias=-255.5 / 512)
+    ac(basea, pf, scale=64.0, bias=1.0 - 64 * R0)
+    ac(da, e127, scale=-5.0, bias=col(3))
+    some(4)
+    ac(R("ident", XO + 256, X1), idn(256), bias=256.0)
+    ac(R("cl", 16, 22), idn(6), scale=16.0, bias=r15)
+    co(R("seg32"), 1.0)
+    some(1)
+    co(R("seg32", 0, 192, every, 32), 0.0)
+    ac(R("cl", 12, 14), idn(2), scale=0.0, bias=r15)
+    ac(R("cl", 14, 16), R("cl", 12, 14), bias=16.0)
+    co(R("w1", 0, 192), 0.0)
+    co(R("Fa"), 0.0)
+
+    st0, bt0 = R("sb", 0, 12, q3), R("sb", 16, 28, q3)
+    la, lb = [R("l0", 12 * i, 12 * i + 12, q3) for i in range(2)]
+    fb, fc, fd, fe = [R("lf", 12 * i, 12 * i + 12, q3) for i in range(4)]
     ts(la, st0, 3, None, A.arith_shift_right)
     ts(lb, bt0, 1, None, A.bitwise_and)
     ts(fb, st0, 2.0, None, A.mult)
     ts(fc, la, -1023.0 / 64, None, A.mult)
     tt(fd, fb, lb, A.add)
-    cp(R("nxf", P=q0), R("nxi", P=q0))
+    fill(R("tba", 768, 896, slice(0, R0)), 4096)
     tt(fe, fd, fc, A.add)
-    turn(R("nxt", P=q0), R("nxf", P=q0))
-    ts(R("lx", 0, 12, q0), fe, 64.0, None, A.mult)
-
-    ac(R("seg"), R("j15"), fn=AF.Sign)
-    ac(R("sg", 0, 189), R("sg", 0, 189), fn=AF.Sign)
-    ac(R("i16"), R("c16", 0, 12), bias=r15)
-    for n in ("xa", "xb"):
-        ac(R(n, 3, 48, every, 4), R("i16"), bias=192.0)
-    for d in range(3):
-        ac(col(8 + d), r15, scale=191.0, bias=15.0 - 192 + C * d)
-    ac(R("ident", 256, 512), R("ident", 0, 256), bias=256.0)
-    ac(R("ident", 512, 1024), R("ident", 0, 512), bias=512.0)
-    ac(R("ident", 1024, 1104), R("ident", 0, 80), bias=1024.0)
-
-    tt(R("n1m"), ind(R("tba"), off0), R("mask2"), A.mult)
-    ts(b2, bt0, 1, None, A.arith_shift_right)
-    cp(stu, sti)
-    scan(R("n1s"), R("seg"), R("n1m"))
-    n1v = ends("n1s", q0)
-    cp(R("stf"), sti)
-    tt(R("E1", P=q0), n1v, b2, A.add)
-    for q in range(4):
-        ts(R("t1", P=Qd[q]), n1v, 1.0 / 1024, -255.5 / 512, A.mult, A.add)
-    cp(R("M1", P=QM), R("E1", P=q0))
-    send("ma", lambda k: R("M1"))
-    co(R("tb", 0, 4), 4096.0)
-    co(R("tb", 1028, 1032), 4096.0)
+    fill(R("tba", 896, 1024, slice(0, R0)), 4096)
+    for j, i in enumerate((0, 2, 1, 3)):
+        ts(R("la", j, 12, q3, 4), R("lf", 36 + i, 48, q3, 4), 64.0, None, A.mult)
+    fill(R("xs", 0, 32), 0.0)
+    ts(R("GA"), ind(R("tba"), R("la")), s1, s2, A.mult, A.add)
+    for h in range(2):
+        ts(R("LM", 6 + h, 12, QM, 2), R("sb", 2 + h, 14, q3, 4), float(XO), None, A.add)
+    ac(R("val1"), ind(R("ident"), R("LM", 6, 12)), bias=float(XO - ZC))
+    some(99)
+    ts(R("eqa", P=q3), R("GA", P=q3), col(9, q3), None, A.is_equal)
+    turn(R("GT", P=q3), R("GA", P=q3))
+    scan(R("cua", P=q3), R("eqa", P=q3), R("eqa", P=q3), col(8, q3), A.max, A.add)
+    for h in range(2):
+        ts(R("b2", h, 6, q3, 2), R("sb", 18 + h, 30, q3, 4), 1, None, A.arith_shift_right)
+    scan(R("za", P=q3), R("cua", P=q3), R("eqa", P=q3), 0.0, A.max, A.mult)
+    tt(R("E1", P=q3), R("GT", 31, 192, q3, 32), R("b2", P=q3), A.add)
+    fill(R("M1", 0, 6), 0)
+    turn(R("zt", P=q3), R("za", P=q3))
+    cp(R("M1", 6, 12), R("cl", 16, 22))
+    cp(R("M1", 0, 6, QM), R("E1", P=q3))
+    scan(R("zs", P=q3), R("seg32", P=q3), R("zt", P=q3))
+    qx(0)
+    ts(R("M1", 6, 12, QM), R("zs", 31, 192, q3, 32), -2.0, None, A.add)
+    send(("ma", lambda k: R("M1")))
+    D("y", R("land", rank, rank + 1), R("nxt", 0, 16, lower), "dto", outap=T.land[rank, 0:64, :])
     for i in range(8):
-        for h in range(2):
-            D("y", R("tb", 4 + 512 * h, 516 + 512 * h, slice(i, i + 1)), R("nxt", 32 * h, 32 * h + 16, q0), "dtr", i == 7 and h == 1)
-    D("y", R("xs", 2 * X0, 4 * X0), None, "dx1", inap=T.x[:, 2 * X0 - 4 * Z0:2048])
-    for i in range(1, 16):
-        D("y", R("tb", 4, 1028, slice(8 * i, 8 * i + 8)), R("tb", 4, 1028, slice(0, 8)), "dtq", i == 15)
-    D("y", R("ws", 0, 1024), None, "dw0", inap=T.w[:, 0:1024])
+        D("y", R("tab", P=slice(16 * i, 16 * i + 1)), R("land", 0, 4), "dtr", i == 7, inap=T.land[:, 0:64, :])
 
-    ac(R("val1"), ind(idn, stu), bias=float(Z0))
-    co(R("w1", 0, 192), 0.0)
+    ac(col(16), col(13), scale=-1.0, bias=1.0)
+    ac(col(17), col(13), scale=12.0, bias=col(10))
+    co(R("K"), -1.0)
+    for h in range(2):
+        ac(R("cl", h, 12, every, 2), idn(6), scale=col(16), bias=col(17))
+    co(R("K", 0, 192, every, 16), 0.0)
+    for k in range(3):
+        co(R("K", 8 - k, 192, every, 32), 4.0 * rank + to[k])
+        co(R("K", 24 - k, 192, every, 32), 4.0 * frm[k] + rank)
+    co(R("K", 5, 192, every, 32), float(rank))
+    co(R("XV"), 0.0)
+    co(R("one"), 1.0)
+    ac(col(18), r15, bias=col(14))
+    ac(col(21), qf, bias=1.0)
+    ac(col(19), col(12), scale=float(XO - ZC))
+    co(R("g3", 0, 3), 0.0)
+    ac(R("g3", 3, 4), r15, scale=-64.0, bias=511.0)
+    ac(R("cl", 22, 28, every, 2), idn(3), scale=64.0, bias=1.0)
+    ac(R("cl", 23, 28, every, 2), idn(3), scale=64.0, bias=17.0)
+    ac(col(20), col(11), scale=float(X1 - ZC), bias=col(19))
 
-    def classes(t, eq, s, bb, bt, rr, pp, xx, kc, cross, fillers):
-        def part(name, j, n=12):
-            return R(name, n * j, n * j + n)
-
-        def gap():
-            if fillers:
-                fillers.pop(0)()
-        gap()
-        for j, d in enumerate(oth):
-            ts(part(eq, j), t, float(d), -16.0, A.is_equal, A.add)
-        gap()
-        scan(R(s), R("sg", 0, 36), R(eq, 0, 36))
-        ac(R(eq, 36, 72), R(eq, 0, 36), bias=16.0)
-        if cross:
-            for a, b, n, c, v in ((64, 32, 32, 2, 0), (32, 0, 32, 1, 0), (64, 0, 64, 0, 1), (96, 64, 32, 1, 1), (96, 0, 32, 2, 1)):
-                o, i_ = R("g9", c, 9, slice(a, a + n), 3), R(s, 11, 36, slice(b, b + n), 12)
-                if v:
-                    ts(o, i_, 0.5, None, A.mult)
-                else:
-                    ac(o, i_, scale=0.5)
-            gap()
-            scan(R("g9", 9, 18), R("sg", 132, 141), R("g9", 0, 9))
-        gap()
-        for j in range(3):
-            last = R(s, 12 * j + 11, 12 * j + 12)
-            before = R("g9", 11 + 3 * j, 12 + 3 * j) if cross else None
-            if j == 2 and cross:
-                ac(part(bb, j, 32), R("maskb"), scale=last, bias=before)
-            elif cross:
-                ts(part(bb, j, 32), R("maskb"), last, before, A.mult, A.add)
-            else:
-                ts(part(bb, j, 32), R("maskb"), last, None, A.mult)
-        gap()
-        turn(R(bt), R(bb))
-        gap()
-        scan(R(rr), R("sg", 36, 132), R(bt))
-        gap()
-        for j in range(3):
-            ts(part(pp, j), part(s, j), R(rr, 32 * j + 31, 32 * j + 32), col(kc + j), A.add, A.add)
-        gap()
-        for j in range(3):
-            tt(R(xx, j, 48, every, 4), part(pp, j), part(eq, 3 + j), A.mult)
-        gap()
-        scan(R(xx, 48, 96), R("sg", 141, 189), R(xx, 0, 48))
-        return R(xx, 51, 96, every, 4)
-
-    def own():
-        ts(R("off", P=QM), R("E1", P=q0), 4.0 - 1024 * rank, 1028.0, A.add, A.min)
-
-    def qx(i):
-        return lambda: quant(R("QX", 130 * i, 130 * i + 130), R("SX", 130 * i, 130 * i + 130), R("xs", 520 * i, 520 * i + 520))
-
-    def wq(i):
-        return lambda: quant(R("WQ", 128 * i, 128 * i + 128), R("WS", 128 * i, 128 * i + 128), R("ws", 512 * i, 512 * i + 512))
-
-    z1 = classes(R("t1"), "eqa", "sa", "ba", "bta", "ra", "pa", "xa", 8, False,
-                 [own, lambda: ts(R("maskc"), R("ident", 0, 32), p31, None, A.is_gt), lambda: None] + [qx(i) for i in range(4)])
-    slot1 = R("sl", 0, 12)
-    cp(slot1, z1)
-    ac(R("MP"), z1)
-    send("mp", lambda k: R("MP"))
-    ac(od, ev, scale=-1.0, bias=1.0)
-    ac(col(6), ev, scale=float(Z0))
-    ac(col(7), qf, scale=524288.0)
-    ac(col(15), col(7), scale=od)
-    for d in range(3):
-        ac(col(11 + d), qf, scale=3072.0, bias=col(8 + d))
-    ac(R("park"), R("i16"), bias=288.0)
-    ac(R("K2"), R("i16"), scale=od, bias=col(6))
-    co(R("g9", 0, 9), 0.0)
-    ac(R("L0f", P=QM), R("stf", P=QM), bias=float(Z0))
-    co(R("w2", 0, 192), 0.0)
-
-    scatter(R("w1"), slot1, R("val1"))
-    tt(R("f1", 0, 192), R("w1", 0, 192), R("mask"), A.mult)
-    for k, d in enumerate(oth):
-        ts(R("off", P=Qd[d]), R("A1", 12 * k, 12 * k + 12, Qd[d]), 4.0 - 1024 * rank, 1028.0, A.add, A.min)
-    scan(R("f1", 192, 384), R("seg"), R("f1", 0, 192))
-    ts(R("c1i"), R("off"), 0.5, Z0 - 2.25, A.mult, A.add)
-    cp(R("stl"), ends("f1", a=192))
-    tt(R("n2m"), ind(R("tb"), R("off")), R("mask"), A.mult)
+    qx(1)
+    scatter(R("w1"), R("M1", 6, 12), R("val1"))
+    qx(2)
+    turn(R("wt", P=QM), R("w1", 0, 192, QM))
+    qx(3)
+    for q in range(4):
+        tt(R("Fa", 0, 6, Qd[q]), R("wt", 0, 192, QM, 32), R("wt", 16, 192, QM, 32), A.add)
+    cp(R("cu", 12, 16), R("cl", 12, 16))
+    turn(R("Ta"), R("Fa"))
+    cp(R("LM", 0, 6, QM), R("E1", P=q3))
+    dup = R("cu", 12, 16)
+    cp(R("Za"), ind(R("Ta"), dup))
+    cp(R("cu", 0, 12), R("cl", 0, 12))
+    turn(R("La"), R("Za"))
+    fill(R("kw", 12, 13), 0)
+    for h in range(2):
+        ts(R("stl", h, 12, every, 2), R("La", 32 * h, 32 * h + 6), float(ZC), None, A.add)
     pickq(R("Q1"), R("QX"), R("stl"))
     picks(R("S1"), R("SX"), R("stl"))
-    D("s", R("ws", 1024, 3072), None, "dw1", inap=T.w[:, 1024:3072])
-    send("qa", block("Q1"), True)
-    send("sa", block("S1"))
-    D("y", R("W1", 0, X0), R("QX"), "dq1", False, outap=u8(ap(R("W1", 0, X0))), inap=u8(ap(R("QX"))))
-    D("y", R("P1", 0, X0), R("SX"), "dq1")
-    D("y", R("W2", 0, X1), R("W1", 0, X1), "dq2", False, outap=u8(ap(R("W2", 0, X1))), inap=u8(ap(R("W1", 0, X1))))
-    D("y", R("P2", 0, X1), R("P1", 0, X1), "dq2")
-    scan(R("n2s"), R("seg"), R("n2m"))
-    cp(R("c1u"), R("c1i"))
-    n2v = ends("n2s")
-    ts(R("t2"), n2v, 1.0 / 512, -255.5 / 512, A.mult, A.add)
-    ac(R("uf1"), ind(idn, R("c1u")), scale=2048.0)
-    ac(R("n2k"), n2v, scale=2048.0, bias=float(X1))
-    z2 = classes(R("t2"), "eqb", "sc", "bb", "btb", "rb", "pb", "xb", 11, True,
-                 [lambda: ts(R("c1o"), R("c1i"), od, float(-X1), A.mult, A.add), wq(0), wq(1)])
-    for k, d in enumerate(oth):
-        ac(R("L0f", P=Qd[d]), R("AP", 12 * k, 12 * k + 12, Qd[d]), bias=float(X0))
-    ac(R("L0e"), R("L0f"), scale=ev)
-    tt(R("M2"), R("n2k"), z2, A.add)
-    send("mz", lambda k: R("M2"))
-    slot2 = R("sl", 12, 24)
-    cp(slot2, z2)
-    cp(R("L0u"), R("L0f"))
-    tt(R("val2"), ind(idn, R("L0u")), R("uf1"), A.add)
-    wq(2)()
-    scatter(R("w2"), slot2, R("val2"))
-    tt(R("SBm"), R("L0e"), R("c1o"), A.add)
-    co(R("pw", 0, 288), 0.0)
-    co(R("PZ"), 0.0)
-    co(R("g3", 0, 3), 0.0)
-    co(R("F32"), 0.0)
-    near, far0, far1 = sorted(range(N - 1), key=lambda k: topo.chip(cores[oth[k]]) != topo.chip(core))
-    tc = [R("tc", 32 * i, 32 * i + 32) for i in range(7)]
+    send(("qa", block("Q1")), codes=True)
+    send(("sa", block("S1")))
+    copy("W1", "P1", ZC, X1, "QX", "SX", "dq1")
+    wait("y", [left["sa"]])
+    for i in range(1, 3):
+        D("y", R("ws", 1024 * i, 1024 * i + 1024), None, "dw%d" % i, inap=T.w[:, 1024 * i:1024 * i + 1024])
+    copy("W2", "P2", ZC, X1, "QX", "SX", "dq2")
+    copy("W2", "P2", 0, ZC, "W1", "P1", "dq3")
 
-    def s0():
-        tt(R("f2", 0, 192), R("w2", 0, 192), R("mask"), A.mult)
+    ac(R("XV", 4, 96, every, 16), idn(6), scale=0.0, bias=col(21))
+    ac(R("XV", 3, 96, every, 16), R("cl", 22, 28), bias=col(18))
+    ac(R("identC"), idn(512), scale=col(12), bias=col(20))
+    for a in (0, 240):
+        co(R("pw", a, a + 240), 0.0)
+    for n in ("Fs", "Fp"):
+        co(R(n), 0.0)
+    ac(R("identR", 0, 192), idn(192), scale=col(11))
+    co(R("identR", 192, 200), 0.0)
 
-    def e0():
-        tt(R("Zf", 0, 12), R("n2k"), R("SBm"), A.add)
+    for k, d in enumerate(frm):
+        cp(R("LM", P=Qd[d]), R("A1", 12 * k, 12 * k + 12, Qd[d]))
+    cp(R("GB"), ind(R("tab"), R("LM", 0, 6)))
+    e1, at = R("LM", 0, 6), R("LM", 6, 12)
+    ts(R("vi", 0, 6), e1, 1.0 / 1024, -511.5 / 1024, A.mult, A.add)
+    ts(R("vi", 6, 12), e1, 0.5, XO - X1 - 512.0 * rank - 0.25, A.mult, A.add)
+    turn(R("PT"), R("GB"))
+    ts(R("vf", 0, 6), R("vi", 0, 6), float(rank), None, A.is_equal)
+    ts(R("vf", 6, 12), at, -float(X1), None, A.add)
+    pv = R("PT", 0, 96, every, 16)
+    ts(R("kw", 0, 6), pv, 9, None, A.arith_shift_right)
+    ts(R("kw", 6, 12), pv, 9, 3, A.arith_shift_right, A.bitwise_and)
+    ts(R("c2"), pv, 511, None, A.bitwise_and)
+    tt(R("X"), ind(R("kw", 0, 13), R("cu", 0, 12)), R("K"), A.not_equal)
+    tt(R("XV", 0, 96, every, 16), R("vi", 6, 12), R("vf", 0, 6), A.mult)
+    tt(R("XV", 1, 96, every, 16), R("vf", 6, 12), R("vf", 0, 6), A.mult)
+    turn(R("XT"), R("X"))
+    cp(R("c2u"), R("c2"))
+    scan(R("cb"), R("one"), R("XT"), 0.0, A.add, A.subtract)
+    turn(R("V0"), R("XV"))
+    for a, b, n, c, v in ((32, 0, 32, 1, 0), (64, 32, 32, 2, 0), (64, 0, 64, 0, 1), (96, 64, 32, 1, 1), (96, 0, 32, 2, 1)):
+        (cp if v else ac)(R("g3", c, c + 1, slice(a, a + n)), R("cb", 191, 192, slice(b, b + n)))
+    tt(R("V1"), ind(R("identC"), R("c2u")), R("V0"), A.add)
+    scan(R("g3", 4, 8), R("seg32", 1, 5), R("g3", 0, 4))
+    ts(R("cub"), R("cb"), R("g3", 7, 8), None, A.add)
+    wq(0)
+    turn(R("zu"), R("cub"))
+    wq(1)
+    scan(R("zv"), R("X"), R("zu"), 0.0, A.mult, A.max)
+    cp(R("sl", 0, 6), R("zv", 15, 192, every, 32))
+    ts(R("sl", 6, 12), R("zv", 31, 192, every, 32), 192.0, None, A.min)
+    scatter(R("pw"), R("sl", 0, 6), R("V1"))
+    tt(R("val"), ind(R("identR"), R("sl", 6, 12)), R("V1"), A.add)
 
-    def s1():
-        scan(R("f2", 192, 384), R("seg"), R("f2", 0, 192))
-        wq(3)()
-
-    def e1():
-        tt(R("Zf", 12, 24), R("Zf", 0, 12), landed("mz", near), A.min)
-
-    def s2():
+    def fold(s, a, n, lists, extra, gaps):
+        def gap():
+            if gaps:
+                gaps.pop(0)()
+        F_, H_, G_, T_, U_, S_, Z_, L_ = [x + s for x in "FHGTUSZL"]
+        turn(R("T1", a, a + 32 * n), R("pw", a, a + 32 * n))
+        gap()
+        for j, k in enumerate(lists + extra):
+            c = n * j if j < len(lists) else 32 + n * (j - len(lists))
+            tt(R(F_, c, c + n), R("T1", a + k, a + 32 * n, every, 32), R("T1", a + 16 + k, a + 32 * n, every, 32), A.add)
+        gap()
         for q in (1, 3, 0, 2):
-            (ac if q % 2 else cp)(R("hg", 0, 12, Qd[q]), ends("f2", Qd[q ^ 1], a=192))
-
-    def e2():
-        tt(R("Zf", 24, 36), landed("mz", far0), landed("mz", far1), A.min)
-
-    def s3():
-        tt(R("hg", 12, 24), ends("f2", a=192), R("hg", 0, 12), A.add)
-
-    def e3():
-        tt(R("Zi", 0, 12), R("Zf", 24, 36), R("Zf", 12, 24), A.min)
-
-    def s4():
-        ac(R("hg", 24, 36, upper), R("hg", 12, 24, lower))
-        cp(R("hg", 24, 36, lower), R("hg", 12, 24, upper))
-
-    def e4():
-        ts(R("Zi", 12, 24), R("Zi", 0, 12), 20, None, A.arith_shift_right)
-        ts(R("Zi", 24, 36), R("Zi", 0, 12), 11, 511, A.arith_shift_right, A.bitwise_and)
-        ts(R("Zi", 36, 48), R("Zi", 0, 12), 2047, None, A.bitwise_and)
-
-    def s5():
-        tt(R("fa", 0, 12), R("hg", 12, 24), R("hg", 24, 36), A.add)
-
-    def e5():
-        ts(R("PZ", 0, 12), R("Zi", 12, 24), float(rank), None, A.is_equal)
-        ac(R("pr"), R("PZ", 0, 12), scale=-1024.0)
-        ts(R("ze", 0, 12), R("Zi", 24, 36), ev, None, A.mult)
-
-    def s6():
-        ts(R("l34", 0, 12), R("fa", 0, 12), 1.0 / 2048, None, A.mult)
-        ts(R("fa", 24, 36), R("fa", 0, 12), 2047, None, A.bitwise_and)
-
-    def e6():
-        turn(tc[0], R("PZ"))
-        tt(R("ze", 12, 24), R("ze", 0, 12), R("K2"), A.add)
-
-    def s7():
-        cp(R("l34", 12, 24), R("fa", 24, 36))
-
-    def e7():
-        scan(tc[1], R("seg", 0, 32), tc[0])
-        cp(R("zl", 12, 24), R("ze", 12, 24))
-
-    def s8():
-        pickq(R("Q3"), R("QX"), R("l34", 0, 12))
-        picks(R("S3"), R("SX"), R("l34", 0, 12))
-        send("qb", block("Q3"), True)
-
-    def e8():
-        for a, b, n, c, v in ((32, 0, 32, 1, 0), (64, 32, 32, 2, 0), (64, 0, 64, 0, 1), (96, 64, 32, 1, 1), (96, 0, 32, 2, 1)):
-            (cp if v else ac)(R("g3", c, c + 1, slice(a, a + n)), R("tc", 47, 48, slice(b, b + n)))
-        tt(R("pz", 0, 12), R("park"), R("pr"), A.add)
-
-    def e9():
-        scan(R("g3", 3, 6), R("sg", 132, 135), R("g3", 0, 3))
-        ac(R("uf2"), ind(idn, R("zl", 12, 24)), scale=2048.0, bias=col(15))
-
-    def s9():
-        pickq(R("Q4"), R("W1", 0, X1), R("l34", 12, 24))
-        picks(R("S4"), R("P1", 0, X1), R("l34", 12, 24))
-        send("sb", block("S3"))
-        send("qc", block("Q4"), True)
-        send("sc", block("S4"))
-
-    for fn in (s0, e0, s1, s2, e1, s3, e2, s4, e3, s5, e4, s6, e5, s7, e6, s8, e7, e8, e9, s9):
-        fn()
-    cp(R("zl", 0, 12), R("Zi", 36, 48))
-    ts(tc[2], R("maskc"), R("tc", 47, 48), R("g3", 5, 6), A.mult, A.add)
-    turn(tc[3], tc[2])
-    wq(4)()
-    scan(tc[4], R("sg", 36, 68), tc[3])
-    wq(5)()
-    ts(tc[5], tc[1], R("tc", 159, 160), -1.0, A.add, A.add)
-    turn(tc[6], tc[5])
-    tt(R("val3"), ind(idn, R("zl", 0, 12)), R("uf2"), A.add)
-    tt(R("pz", 12, 24), R("tc", 192, 204), R("pz", 0, 12), A.max)
-    slot3 = R("sl", 24, 36)
-    cp(slot3, R("pz", 12, 24))
-    scatter(R("pw"), slot3, R("val3"))
-    turn(R("f3"), R("pw", 0, 288))
-    for q in (1, 3, 0, 2):
-        (ac if q % 2 else cp)(R("hm", P=Qd[q]), R("f3", 0, 288, Qd[q ^ 1], 16))
-    for k in range(2):
-        tt(R("F32", 16 * k, 16 * k + 9), R("f3", 16 * k, 288, every, 32), R("hm", k, 18, every, 2), A.add)
-    turn(R("TF"), R("F32"))
-    ac(R("hx", P=upper), R("TF", P=lower))
-    cp(R("hx", P=lower), R("TF", P=upper))
-    for i in range(4):
-        h = i // 2
-        tt(R("DD", 16 * i, 16 * i + 16), R("TF", h, 32, every, 2), R("hx", h, 32, every, 2), A.add)
-    turn(R("LT"), R("DD"))
-    tt(R("SS"), R("TF"), R("hx"), A.add)
-    ts(R("HU"), R("LT"), 1.0 / 2048, None, A.mult)
-    ts(R("li"), R("LT"), 2047, None, A.bitwise_and)
-    ts(R("idi", 0, 32), R("SS"), 19, None, A.arith_shift_right)
-    ts(R("idi", 32, 64), R("SS"), 11, 255, A.arith_shift_right, A.bitwise_and)
-    ts(R("idi", 64, 96), R("SS"), 1.0, -1.0, A.is_ge, A.add)
-
-    def products(i, q, s, h):
-        for o in range(O):
-            c, d = 128 * ((2 - i) * O + o), 512 * (2 * o + h)
-            a, b = L * h, L * h + L
-            E("t", [R(q, a, b), R(s, a, b), R("WQ", c, c + 128), R("WS", c, c + 128)], [R("ps", d, d + L)] if i == 2 else [],
-              lambda e: e.matmul_mx(ap(R("ps", d, d + L)), ap(R("WQ", c, c + 128)), ap(R("WS", c, c + 128)), ap(R(q, a, b)), ap(R(s, a, b)), i == 0, i == 2))
-
-    for i, (q, s, w, p, l, a) in enumerate((("G2", "H2", R("QX"), R("SX"), "HU", 0), ("G1", "H1", R("W1"), R("P1"), "LU", 16), ("G0", "H0", R("W2"), R("P2"), "LU", 0))):
+            (ac if q % 2 else cp)(R(H_, P=Qd[q]), R(F_, P=Qd[q ^ 1]))
+        gap()
+        tt(R(G_), R(F_), R(H_), A.add)
+        gap()
+        turn(R(T_), R(G_))
+        turn(R(U_, P=upper), R(G_, P=lower))
+        turn(R(U_, P=lower), R(G_, P=upper))
+        gap()
+        tt(R(S_), R(T_), R(U_), A.add)
+        gap()
+        cp(R(Z_), ind(R(S_, 0, 32), dup))
+        gap()
+        turn(R(L_), R(Z_))
+        gap()
+        m = n * len(lists)
         for h in range(2):
-            lst = R(l, 32 * h + a, 32 * h + a + 9)
-            pickq(R(q, L * h, L * h + L), w, lst)
-            picks(R(s, L * h, L * h + L), p, lst)
-            products(i, q, s, h)
-            if i == 0 and h == 0:
-                cp(R("LU"), R("li"))
-    tt(R("idt", 0, 32), R("idi", 0, 32), R("idi", 64, 96), A.add)
-    tt(R("idt", 32, 64), R("idi", 32, 64), R("idi", 64, 96), A.add)
-    for h in range(2):
-        cp(R("ysb", h, M, every, 2), R("ps", 512 * h, 512 * h + L))
-        ac(R("ysb", M + h, 2 * M, every, 2), R("ps", 1024 + 512 * h, 1024 + 512 * h + L))
-    for o in range(2):
-        D("y", None, R("idt", 32 * o, 32 * o + 32, slice(16, 25)), "di%d" % o, outap=T.id[o:o + 1, :])
-    D("y", None, R("ysb", 0, M), "dy0", outap=T.y[:, 0:M])
-    D("s", None, R("ysb", M, 2 * M), "dy1", outap=T.y[:, M:2 * M])
+            ts(R("l" + s, h, 2 * m, every, 2), R(L_, 32 * h, 32 * h + m), float(ZC), None, A.add)
 
-    wait("g", [(q, cnt[q]) for q in ("v", "s", "t", "g")] + [("loc", loc[0])] + [(s, dsum[s]) for s in DMAS] + arrivals)
+    def nop():
+        pass
+
+    fold("s", 0, 6, [0, 1], [], [])
+    pickq(R("Q3"), R("QX"), R("ls", 0, 12))
+    picks(R("S3"), R("SX"), R("ls", 0, 12))
+    send(("qb", block("Q3")), codes=True)
+    pickq(R("Q4"), R("W1", 0, X1), R("ls", 12, 24))
+    picks(R("S4"), R("P1", 0, X1), R("ls", 12, 24))
+    send(("sb", block("S3")), ("sc", block("S4")))
+    send(("qc", block("Q4")), codes=True)
+    scatter(R("pw"), R("sl", 0, 6), R("val"))
+    wq(2)
+    fold("p", 192, 9, [0, 1, 2], [3, 4], [nop, nop, lambda: wq(3), nop, nop, lambda: wq(4), nop, lambda: wq(5)])
+    ac(R("idt"), R("Sp", 32, 64), bias=-1.0)
+    D("y", None, R("idt", P=slice(9, 18)), "di0", outap=T.id[0:1, :])
+    D("y", None, R("idt", P=slice(0, 9)), "di1", outap=T.id[1:2, :])
+
+    for i, (q, s, w, p, l) in enumerate((("G2", "H2", "QX", "SX", 36), ("G1", "H1", "W1", "P1", 0), ("G0", "H0", "W2", "P2", 18))):
+        for h, (a, b) in enumerate(PARTS):
+            lst = R("lp", l + a // 16, l + b // 16)
+            pickq(R(q, a, b), R(w), lst)
+            picks(R(s, a, b), R(p), lst)
+            for o in range(O):
+                c, d = 128 * ((2 - i) * O + o), 512 * (2 * o + h)
+                out = R("ps", d, d + b - a)
+                E("t", [R(q, a, b), R(s, a, b), R("WQ", c, c + 128), R("WS", c, c + 128)], [out] if i == 2 else [],
+                  lambda e: e.matmul_mx(ap(out), ap(R("WQ", c, c + 128)), ap(R("WS", c, c + 128)), ap(R(q, a, b)), ap(R(s, a, b)), i == 0, i == 2))
+    for h, (a, b) in enumerate(PARTS):
+        cp(R("ysb", a, b), R("ps", 512 * h, 512 * h + b - a))
+        ac(R("ysb", M + a, M + b), R("ps", 1024 + 512 * h, 1024 + 512 * h + b - a))
+        D("y", None, R("ysb", a, b), "dy0", h == 1, outap=T.y[:, a:b])
+        D("y", None, R("ysb", M + a, M + b), "dy1", h == 1, outap=T.y[:, M + a:M + b])
+
+    wait("g", [(q, cnt[q]) for q in ("v", "s", "t", "g")] + [left[h] for h in CALLS] + [(s, dsum[s]) for s in DMAS] + arrivals)

@@ -7,8 +7,12 @@ ZC = 192
 XO = 200
 X1 = XO + 512
 R0 = 123
-PARTS = ((0, 160), (160, 288))
-F, I, U, B = "float32", "int32", "uint16", "bfloat16"
+PARTS = ((0, 128), (128, 288))
+WEAVE = "zutglLqdhC memmmmvmcmm1mmmmmmamA sxssysspspspspss ppppwpwpwpwpwpwp"
+FAV = 3
+OPT = (0, 0, "")
+TB = 768
+F, I, U, B, H = "float32", "int32", "uint16", "bfloat16", "float16"
 Q8, S8 = "float8_e4m3fn_x4", "uint8"
 
 
@@ -17,30 +21,32 @@ def _sb(w, d):
 
 
 SCRATCH = {
-    "tba": _sb(1024, I), "tab": _sb(4096, F), "land": ("dram", [4, 128, 16], F), "sb": _sb(32, I), "nxi": _sb(32, I), "nxf": _sb(32, F), "nxt": _sb(32, F),
+    "tba": _sb(1024, I), "land": ("dram", [4, 128, 8], I), "sb": _sb(40, I),
+    "seg16": _sb(96, F), "OU": _sb(4, F), "UB": _sb(96, F), "PS": _sb(96, F), "A2": _sb(36, B), "MP": _sb(12, B),
     "xs": _sb(4 * 520, B), "ws": _sb(3072, B),
     "QX": _sb(X1, Q8), "SX": _sb(X1, S8), "W1": _sb(X1 + 192, Q8), "P1": _sb(X1 + 192, S8), "W2": _sb(X1 + 192, Q8), "P2": _sb(X1 + 192, S8),
-    "WQ": _sb(768, Q8), "WS": _sb(768, S8),
+    "WQ": _sb(768, Q8), "WS": _sb(768, S8), "OH": _sb(16, F),
     "Q1": _sb(192, Q8), "S1": _sb(192, S8), "Q3": _sb(192, Q8), "S3": _sb(192, S8), "Q4": _sb(192, Q8), "S4": _sb(192, S8),
     "G0": _sb(288, Q8), "H0": _sb(288, S8), "G1": _sb(288, Q8), "H1": _sb(288, S8), "G2": _sb(288, Q8), "H2": _sb(288, S8),
     "pI": _sb(2, I), "ci": _sb(8, I), "cf": _sb(32, F), "ident": _sb(X1, F), "identC": _sb(512, F), "identR": _sb(200, F),
-    "seg32": _sb(192, F), "one": _sb(192, B), "K": _sb(192, F), "cl": _sb(32, F), "cu": _sb(16, U),
-    "l0": _sb(36, I), "lf": _sb(48, F), "la": _sb(12, U), "b2": _sb(6, I),
-    "GA": _sb(192, I), "GT": _sb(192, I), "eqa": _sb(192, F), "cua": _sb(192, F), "za": _sb(192, F), "zt": _sb(192, F), "zs": _sb(192, F),
-    "E1": _sb(6, F), "M1": _sb(12, U), "A1": _sb(36, U), "LM": _sb(12, U), "val1": _sb(96, F), "w1": _sb(384, F), "wt": _sb(192, F),
+    "seg32": _sb(192, B), "one": _sb(192, B), "K": _sb(192, F), "cl": _sb(40, F), "cu": _sb(16, U),
+    "l0": _sb(36, I), "lf": _sb(72, F), "ul": _sb(40, U), "b2": _sb(6, I),
+    "GA": _sb(192, I), "GT": _sb(192, I), "eqa": _sb(192, B), "cua": _sb(192, H), "za": _sb(192, H), "zt": _sb(192, H), "zs": _sb(192, H),
+    "E1": _sb(6, F), "A1": _sb(36, U), "val1": _sb(96, F), "w1": _sb(384, F), "wt": _sb(192, F),
     "Fa": _sb(32, F), "Ta": _sb(32, F), "Za": _sb(64, F), "La": _sb(64, F), "stl": _sb(12, U),
-    "GB": _sb(96, I), "PT": _sb(96, I), "kw": _sb(16, I), "c2": _sb(6, I), "c2u": _sb(6, U), "vi": _sb(12, I), "vf": _sb(12, F),
+    "GB": _sb(96, F), "PT": _sb(96, F), "kw": _sb(32, I), "c2u": _sb(6, U), "vi": _sb(12, I),
     "XV": _sb(96, F), "V0": _sb(96, F), "V1": _sb(96, F), "val": _sb(96, F),
-    "X": _sb(192, B), "XT": _sb(192, B), "cb": _sb(192, B), "g3": _sb(8, F), "cub": _sb(192, F), "zu": _sb(192, F), "zv": _sb(192, F),
+    "X": _sb(192, B), "XT": _sb(192, B), "cb": _sb(192, B), "g3": _sb(8, F), "cub": _sb(192, H), "zu": _sb(192, H), "zv": _sb(192, H),
     "sl": _sb(12, U), "pw": _sb(1280, F), "T1": _sb(480, F),
     "Fs": _sb(32, F), "Hs": _sb(32, F), "Gs": _sb(32, F), "Ts": _sb(32, F), "Us": _sb(32, F), "Ss": _sb(32, F), "Zs": _sb(64, F), "Ls": _sb(64, F), "ls": _sb(24, U),
     "Fp": _sb(64, F), "Hp": _sb(64, F), "Gp": _sb(64, F), "Tp": _sb(64, F), "Up": _sb(64, F), "Sp": _sb(64, F), "Zp": _sb(64, F), "Lp": _sb(64, F), "lp": _sb(54, U),
     "idt": _sb(32, F), "ysb": _sb(576, F),
     "ps": ("psum", [128, 2048], F),
 }
-DMAS = ["dnx", "dst", "dx", "dx1", "dw0", "dw1", "dw2", "dni", "dto", "dtr", "dq1", "dq2", "dq3", "dy0", "dy1", "di0", "di1"]
-HOPS = ("nt", "ma", "qa", "sa", "qb", "qc", "sb", "sc")
-CALLS = ("nt", "ma", "qa", "sa", "qb", "qc", "sb")
+LISTS = {"la": (0, 12), "LM": (12, 28)}
+DMAS = ["dnx", "dst", "dx", "dx1", "dw0", "dw1", "dw2", "dto", "dtr", "dq1", "dq2", "dq3", "dy0", "dy1", "di0", "di1"]
+HOPS = ("nt", "ma", "mp", "qa", "sa", "qb", "qc", "sb", "sc")
+CALLS = ("nt", "ma", "mp", "qa", "sa", "qb", "qc", "sb")
 SEMAPHORES = ["v", "s", "t", "g"] + DMAS + [n + str(k) for n in HOPS for k in range(N - 1)] + ["l" + n for n in CALLS]
 
 
@@ -77,6 +83,8 @@ def rank_program(g, core, T, topo):
     QM, q3 = Qd[rank], Qd[3]
 
     def R(name, a=0, b=None, P=every, st=1):
+        if name in LISTS:
+            return ("ul", P.start, P.stop, LISTS[name][0] + a, LISTS[name][0] + (LISTS[name][1] if b is None else b), st)
         return (name, P.start, P.stop, a, SCRATCH[name][1][1] if b is None else b, st)
 
     def ind(win, off):
@@ -153,7 +161,7 @@ def rank_program(g, core, T, topo):
     def u32(v):
         return v.bitcast(dt.uint32)
 
-    land = {"ma": ("A1", 0, 12), "qa": ("W1", 0, C), "sa": ("P1", 0, C), "qb": ("W1", X1, C), "sb": ("P1", X1, C), "qc": ("W2", X1, C), "sc": ("P2", X1, C)}
+    land = {"ma": ("A1", 0, 12), "mp": ("A2", 0, 12), "qa": ("W1", 0, C), "sa": ("P1", 0, C), "qb": ("W1", X1, C), "sb": ("P1", X1, C), "qc": ("W2", X1, C), "sc": ("P2", X1, C)}
 
     def landed(h, k, sender):
         if h == "nt":
@@ -162,7 +170,10 @@ def rank_program(g, core, T, topo):
         return R(n, a + w * k, a + w * k + w)
 
     def share(src, dst, h):
-        es = plan(topo, src, cores)[dst]
+        es = plan(topo, src, cores)
+        if h in ("nt", "ma", "mp"):
+            return es[dst][:min(len(e) for e in es.values())]
+        es = es[dst]
         return es[:len(es) // 2] if h == "sb" else es[len(es) // 2:] if h == "sc" else es
 
     def send(*parts, codes=False):
@@ -179,8 +190,8 @@ def rank_program(g, core, T, topo):
         left[parts[0][0]] = ("l" + parts[0][0], n)
         g.remote_dma_fused(tr, local_sem=T.sem["l" + parts[0][0]])
 
-    def block(n):
-        return lambda k: R(n, C * k, C * k + C)
+    def block(n, w=C):
+        return lambda k: R(n, w * k, w * k + w)
 
     arrivals = []
     for h in HOPS:
@@ -232,11 +243,11 @@ def rank_program(g, core, T, topo):
     def co(out, c):
         ac(out, idn(min(256, len(range(out[3], out[4], out[5]))), slice(out[1], out[2])), scale=0.0, bias=c)
 
-    def iota(out, pattern, cm=0, flag=True):
+    def iota(out, pattern, cm=0, flag=True, base=0):
         if flag:
-            E("g", [], [out], lambda e: e.iota(ap(out), pattern, 0, cm, allow_small_or_imprecise_dtypes=True))
+            E("g", [], [out], lambda e: e.iota(ap(out), pattern, base, cm, allow_small_or_imprecise_dtypes=True))
         else:
-            E("g", [], [out], lambda e: e.iota(ap(out), pattern, 0, cm))
+            E("g", [], [out], lambda e: e.iota(ap(out), pattern, base, cm))
 
     def pickq(out, win, off):
         E("v", [win, off], [out], lambda e: e.tensor_copy(u32(ap(out)), u32(ap(win)).indirect(ap(off))))
@@ -262,68 +273,50 @@ def rank_program(g, core, T, topo):
         D("y", R(p, a, b), R(s, a, b), sem)
 
     g6, g7 = slice(96, 112), slice(112, 128)
-    fill(R("sb", P=q3), 0)
-    fill(R("nxf"), 0.0)
-    for h in range(2):
-        D("ys"[h], R("nxi", P=slice(32 * h, 32 * h + 16)), None, "dni", h == 1, inap=T.nx[:, 32 * h:32 * h + 32])
+    for i in range(2):
+        fill(R("sb", 20 * i, 20 * i + 8, g6), 0)
+    D("y", R("land", rank, rank + 1), None, "dto", inap=T.nx[:])
     for i, t in enumerate((T.st, T.bt)):
-        D("ys"[i], R("sb", 16 * i, 16 * i + 12, g7), None, "dst", False, inap=t[:])
-        D("ys"[i], R("sb", 16 * i + 2, 16 * i + 14, g6), None, "dst", i == 1, inap=t[:])
+        D("ys"[i], R("sb", 20 * i + 2, 20 * i + 14, g7), None, "dst", False, inap=t[:])
+    for i, t in enumerate((T.st, T.bt)):
+        D("ys"[i], R("sb", 20 * i + 8, 20 * i + 20, g6), None, "dst", i == 1, inap=t[:])
     for p in range(R0, 128):
-        D("ys"[p % 2], R("tba", P=slice(p, p + 1)), None, "dnx", p == 127, inap=T.nx[:])
+        D("sy"[p % 2 == 0], R("tba", P=slice(p, p + 1)), None, "dnx", p == 127, inap=T.nx[:])
     D("y", R("xs", 32, 1040), None, "dx", inap=T.x[:, 0:1008])
     D("y", R("xs", 1040, 2080), None, "dx1", inap=T.x[:, 1008:2048])
-    D("y", R("ws", 0, 1024), None, "dw0", inap=T.w[:, 0:1024])
-    iota(R("pI"), [[128 - R0 + 1 + rank, 2]], 1, False)
+    iota(R("ci", 4, 6), [[128 - R0 + 1 + rank, 2]], 1, False)
     iota(idn(256), [[1, 256]])
-    iota(R("tab", 0, 384), [[0, 384]])
+    iota(R("cl", 22, 34), [[4, 2], [8, 3], [0, 2]], base=1)
+    iota(R("tba", TB, 1024, slice(0, R0)), [[0, 1024 - TB]], 0, False, 4096)
+    send(("nt", lambda k: R("land", rank, rank + 1)))
 
-    pi = R("pI", 0, 1)
+    pi = R("ci", 4, 5)
     r15, p31, qf, pf, e127, s1, s2, basea, da = col(0), col(1), col(2), col(4), col(5), col(6), col(7), col(8), col(9)
-    fill(R("la"), 0)
-    fill(R("LM"), XO)
+    fill(R("ul"), XO)
     ts(R("ci", 0, 1), pi, 15, None, A.bitwise_and)
     ts(R("ci", 1, 2), pi, 31, None, A.bitwise_and)
     ts(R("ci", 2, 3), pi, 5, None, A.arith_shift_right)
-    ts(R("ci", 3, 4), R("pI", 1, 2), 3, None, A.bitwise_and)
+    ts(R("ci", 3, 4), R("ci", 5, 6), 3, None, A.bitwise_and)
     ts(e127, pi, 127.0, None, A.is_equal)
-    cp(pf, pi)
-    cp(R("cf", 0, 4), R("ci", 0, 4))
-    fill(R("tba", 0, 384, slice(0, R0)), 4096)
-    ts(col(10), r15, 5.0, 6.0, A.is_equal, A.mult)
-    ts(col(13), r15, 0.0, None, A.is_equal)
-    ts(col(11), r15, 2.0, None, A.is_lt)
-    ts(col(12), r15, 2.0, None, A.is_equal)
-    ts(col(14), p31, 16.0, 32.0, A.is_ge, A.mult)
-    for h in range(2):
-        P = slice(32 * h, 32 * h + 16)
-        ts(R("nxf", P=P), R("nxi", P=P), 2048.0 * rank, None, A.add)
-    fill(R("tba", 384, 512, slice(0, R0)), 4096)
-    turn(R("nxt"), R("nxf"))
-    fill(R("tba", 512, 768, slice(0, R0)), 4096)
-    send(("nt", lambda k: R("nxt", 0, 16)))
-    iota(R("tab", 384, 896), [[0, 512]])
-    junk = [lambda a=a: co(R("tab", a, min(a + 256, 4096)), 0.0) for a in range(896, 4096, 256)]
-
-    def some(n):
-        for i in range(min(n, len(junk))):
-            junk.pop(0)()
+    cp(R("cf", 0, 5), R("ci", 0, 5))
+    lo, tl, at, c0 = [(lambda P=every, a=a: R("LM", a, a + 6, P)) for a in (0, 6, 16, 22)]
+    fill(R("xs", 0, 32), 0.0)
+    fill(R("tba", 0, TB, slice(0, R0)), 4096)
     ac(s1, e127, scale=2.0 - 1.0 / 512, bias=1.0 / 512)
     ac(s2, e127, scale=255.5 / 512, bias=-255.5 / 512)
     ac(basea, pf, scale=64.0, bias=1.0 - 64 * R0)
     ac(da, e127, scale=-5.0, bias=col(3))
-    some(4)
-    ac(R("ident", XO + 256, X1), idn(256), bias=256.0)
     ac(R("cl", 16, 22), idn(6), scale=16.0, bias=r15)
-    co(R("seg32"), 1.0)
-    some(1)
-    co(R("seg32", 0, 192, every, 32), 0.0)
     ac(R("cl", 12, 14), idn(2), scale=0.0, bias=r15)
-    ac(R("cl", 14, 16), R("cl", 12, 14), bias=16.0)
+    ac(R("cl", 14, 16), idn(2), scale=0.0, bias=R("cl", 17, 18))
+    ac(R("ident", XO + 256, X1), idn(256), bias=256.0)
+    co(R("seg32"), 1.0)
     co(R("w1", 0, 192), 0.0)
+    co(R("seg32", 0, 192, every, 32), 0.0)
+    co(R("MP"), 0.0)
     co(R("Fa"), 0.0)
 
-    st0, bt0 = R("sb", 0, 12, q3), R("sb", 16, 28, q3)
+    st0, bt0 = R("sb", 2, 14, q3), R("sb", 22, 34, q3)
     la, lb = [R("l0", 12 * i, 12 * i + 12, q3) for i in range(2)]
     fb, fc, fd, fe = [R("lf", 12 * i, 12 * i + 12, q3) for i in range(4)]
     ts(la, st0, 3, None, A.arith_shift_right)
@@ -331,178 +324,216 @@ def rank_program(g, core, T, topo):
     ts(fb, st0, 2.0, None, A.mult)
     ts(fc, la, -1023.0 / 64, None, A.mult)
     tt(fd, fb, lb, A.add)
-    fill(R("tba", 768, 896, slice(0, R0)), 4096)
+    ts(R("b2", P=q3), R("sb", 28, 34, q3), 1, None, A.arith_shift_right)
     tt(fe, fd, fc, A.add)
-    fill(R("tba", 896, 1024, slice(0, R0)), 4096)
-    for j, i in enumerate((0, 2, 1, 3)):
-        ts(R("la", j, 12, q3, 4), R("lf", 36 + i, 48, q3, 4), 64.0, None, A.mult)
-    fill(R("xs", 0, 32), 0.0)
+    ts(c0(QM), R("sb", 8, 14, q3), float(XO), None, A.add)
+    for a in range(2):
+        ts(R("la", a, 12, q3, 2), R("lf", 36 + 6 * a, 42 + 6 * a, q3), 64.0, None, A.mult)
+    ts(R("OH"), idn(16), r15, None, A.is_equal)
     ts(R("GA"), ind(R("tba"), R("la")), s1, s2, A.mult, A.add)
-    for h in range(2):
-        ts(R("LM", 6 + h, 12, QM, 2), R("sb", 2 + h, 14, q3, 4), float(XO), None, A.add)
-    ac(R("val1"), ind(R("ident"), R("LM", 6, 12)), bias=float(XO - ZC))
-    some(99)
-    ts(R("eqa", P=q3), R("GA", P=q3), col(9, q3), None, A.is_equal)
+    ac(R("val1"), ind(R("ident"), c0()), bias=float(XO - ZC))
+    oh = [R("OH", i, i + 1) for i in range(16)]
+    ac(col(16), oh[4], scale=0.5)
+    ac(col(10), oh[5], scale=-1.0)
+    ac(R("cf", 22, 26), idn(4), scale=col(16))
     turn(R("GT", P=q3), R("GA", P=q3))
-    scan(R("cua", P=q3), R("eqa", P=q3), R("eqa", P=q3), col(8, q3), A.max, A.add)
-    for h in range(2):
-        ts(R("b2", h, 6, q3, 2), R("sb", 18 + h, 30, q3, 4), 1, None, A.arith_shift_right)
-    scan(R("za", P=q3), R("cua", P=q3), R("eqa", P=q3), 0.0, A.max, A.mult)
-    tt(R("E1", P=q3), R("GT", 31, 192, q3, 32), R("b2", P=q3), A.add)
-    fill(R("M1", 0, 6), 0)
-    turn(R("zt", P=q3), R("za", P=q3))
-    cp(R("M1", 6, 12), R("cl", 16, 22))
-    cp(R("M1", 0, 6, QM), R("E1", P=q3))
-    scan(R("zs", P=q3), R("seg32", P=q3), R("zt", P=q3))
-    qx(0)
-    ts(R("M1", 6, 12, QM), R("zs", 31, 192, q3, 32), -2.0, None, A.add)
-    send(("ma", lambda k: R("M1")))
-    D("y", R("land", rank, rank + 1), R("nxt", 0, 16, lower), "dto", outap=T.land[rank, 0:64, :])
+    wait("y", [("v", cnt["v"])])
+    D("y", R("ws", 0, 1024), None, "dw0", inap=T.w[:, 0:1024])
     for i in range(8):
-        D("y", R("tab", P=slice(16 * i, 16 * i + 1)), R("land", 0, 4), "dtr", i == 7, inap=T.land[:, 0:64, :])
+        D("y", R("tba", P=slice(16 * i, 16 * i + 4)), R("land", 0, 4), "dtr", i == 7, inap=T.land[:])
+    n2x, t1 = R("GT", 31, 192, q3, 32), R("GT", 27, 192, q3, 32)
+    ea, eb, ec, ed = [R("lf", 48 + 6 * i, 54 + 6 * i, q3) for i in range(4)]
+    ef, eg = R("l0", 24, 30, q3), R("l0", 30, 36, q3)
+    ts(R("eqa", P=q3), R("GA", P=q3), col(9, q3), None, A.is_equal)
+    ts(eg, n2x, 1023, None, A.bitwise_and)
+    ts(ef, n2x, 4, 63, A.arith_shift_right, A.bitwise_and)
+    scan(R("cua", P=q3), R("eqa", P=q3), R("eqa", P=q3), col(8, q3), A.max, A.add)
+    tt(ea, eg, R("b2", P=q3), A.add)
+    ts(ec, ef, -1023.0 / 64, None, A.mult)
+    scan(R("za", P=q3), R("cua", P=q3), R("eqa", P=q3), 0.0, A.max, A.mult)
+    tt(ed, ea, ec, A.add)
+    cp(tl(QM), t1)
+    turn(R("zt", P=q3), R("za", P=q3))
+    ts(lo(QM), ed, 64.0, None, A.mult)
+    send(("ma", lambda k: R("LM", 0, 12)))
+    cp(R("LM", 12, 22), R("cl", 12, 22))
+    scan(R("zs", P=q3), R("seg32", P=q3), R("zt", P=q3))
+    ts(R("MP", 0, 12, QM, 2), eg, 0.5, -256.0, A.mult, A.add)
+    ts(at(QM), R("zs", 31, 192, q3, 32), -2.0, None, A.add)
+    ts(R("MP", 1, 12, QM, 2), R("zs", 31, 192, q3, 32), -2.0 - ZC, None, A.add)
+    send(("mp", lambda k: R("MP")))
+    iota(R("seg16"), [[0, 6], [8192, 16]])
+    iota(R("kw", 24, 25), [[0, 1]], 0, False)
 
-    ac(col(16), col(13), scale=-1.0, bias=1.0)
-    ac(col(17), col(13), scale=12.0, bias=col(10))
+    ac(col(17), oh[0], scale=100.0, bias=col(10))
     co(R("K"), -1.0)
-    for h in range(2):
-        ac(R("cl", h, 12, every, 2), idn(6), scale=col(16), bias=col(17))
+    ac(R("cl", 0, 12), R("cl", 22, 34), bias=col(17))
     co(R("K", 0, 192, every, 16), 0.0)
+    co(R("K", 5, 192, every, 32), float(rank))
     for k in range(3):
         co(R("K", 8 - k, 192, every, 32), 4.0 * rank + to[k])
         co(R("K", 24 - k, 192, every, 32), 4.0 * frm[k] + rank)
-    co(R("K", 5, 192, every, 32), float(rank))
-    co(R("XV"), 0.0)
-    co(R("one"), 1.0)
-    ac(col(18), r15, bias=col(14))
+    ac(col(14), r15, scale=-5.0, bias=1.0)
     ac(col(21), qf, bias=1.0)
-    ac(col(19), col(12), scale=float(XO - ZC))
-    co(R("g3", 0, 3), 0.0)
+    ac(col(19), oh[2], scale=float(XO - ZC))
+    ac(col(11), oh[0], bias=oh[8])
+    ac(col(18), p31, scale=6.0, bias=col(14))
+    co(R("XV"), 0.0)
     ac(R("g3", 3, 4), r15, scale=-64.0, bias=511.0)
-    ac(R("cl", 22, 28, every, 2), idn(3), scale=64.0, bias=1.0)
-    ac(R("cl", 23, 28, every, 2), idn(3), scale=64.0, bias=17.0)
-    ac(col(20), col(11), scale=float(X1 - ZC), bias=col(19))
-
-    qx(1)
-    scatter(R("w1"), R("M1", 6, 12), R("val1"))
-    qx(2)
-    turn(R("wt", P=QM), R("w1", 0, 192, QM))
-    qx(3)
-    for q in range(4):
-        tt(R("Fa", 0, 6, Qd[q]), R("wt", 0, 192, QM, 32), R("wt", 16, 192, QM, 32), A.add)
-    cp(R("cu", 12, 16), R("cl", 12, 16))
-    turn(R("Ta"), R("Fa"))
-    cp(R("LM", 0, 6, QM), R("E1", P=q3))
-    dup = R("cu", 12, 16)
-    cp(R("Za"), ind(R("Ta"), dup))
-    cp(R("cu", 0, 12), R("cl", 0, 12))
-    turn(R("La"), R("Za"))
-    fill(R("kw", 12, 13), 0)
-    for h in range(2):
-        ts(R("stl", h, 12, every, 2), R("La", 32 * h, 32 * h + 6), float(ZC), None, A.add)
-    pickq(R("Q1"), R("QX"), R("stl"))
-    picks(R("S1"), R("SX"), R("stl"))
-    send(("qa", block("Q1")), codes=True)
-    send(("sa", block("S1")))
-    copy("W1", "P1", ZC, X1, "QX", "SX", "dq1")
-    wait("y", [left["sa"]])
-    for i in range(1, 3):
-        D("y", R("ws", 1024 * i, 1024 * i + 1024), None, "dw%d" % i, inap=T.w[:, 1024 * i:1024 * i + 1024])
-    copy("W2", "P2", ZC, X1, "QX", "SX", "dq2")
-    copy("W2", "P2", 0, ZC, "W1", "P1", "dq3")
-
+    ac(col(20), col(11), scale=1000.0 + X1 - ZC, bias=-1000.0)
+    ac(R("XV", 0, 96, QM, 16), R("MP", 0, 12, QM, 2))
+    ac(R("XV", 8, 96, QM, 16), R("lf", 6, 12, q3), scale=0.5, bias=float(XO - ZC))
     ac(R("XV", 4, 96, every, 16), idn(6), scale=0.0, bias=col(21))
-    ac(R("XV", 3, 96, every, 16), R("cl", 22, 28), bias=col(18))
-    ac(R("identC"), idn(512), scale=col(12), bias=col(20))
-    for a in (0, 240):
-        co(R("pw", a, a + 240), 0.0)
-    for n in ("Fs", "Fp"):
-        co(R(n), 0.0)
-    ac(R("identR", 0, 192), idn(192), scale=col(11))
-    co(R("identR", 192, 200), 0.0)
+    ac(R("XV", 3, 96, every, 16), idn(6), scale=16.0, bias=col(18))
+    co(R("one"), 1.0)
+    co(R("g3", 0, 3), 0.0)
 
-    for k, d in enumerate(frm):
-        cp(R("LM", P=Qd[d]), R("A1", 12 * k, 12 * k + 12, Qd[d]))
-    cp(R("GB"), ind(R("tab"), R("LM", 0, 6)))
-    e1, at = R("LM", 0, 6), R("LM", 6, 12)
-    ts(R("vi", 0, 6), e1, 1.0 / 1024, -511.5 / 1024, A.mult, A.add)
-    ts(R("vi", 6, 12), e1, 0.5, XO - X1 - 512.0 * rank - 0.25, A.mult, A.add)
-    turn(R("PT"), R("GB"))
-    ts(R("vf", 0, 6), R("vi", 0, 6), float(rank), None, A.is_equal)
-    ts(R("vf", 6, 12), at, -float(X1), None, A.add)
-    pv = R("PT", 0, 96, every, 16)
-    ts(R("kw", 0, 6), pv, 9, None, A.arith_shift_right)
-    ts(R("kw", 6, 12), pv, 9, 3, A.arith_shift_right, A.bitwise_and)
-    ts(R("c2"), pv, 511, None, A.bitwise_and)
-    tt(R("X"), ind(R("kw", 0, 13), R("cu", 0, 12)), R("K"), A.not_equal)
-    tt(R("XV", 0, 96, every, 16), R("vi", 6, 12), R("vf", 0, 6), A.mult)
-    tt(R("XV", 1, 96, every, 16), R("vf", 6, 12), R("vf", 0, 6), A.mult)
-    turn(R("XT"), R("X"))
-    cp(R("c2u"), R("c2"))
-    scan(R("cb"), R("one"), R("XT"), 0.0, A.add, A.subtract)
-    turn(R("V0"), R("XV"))
-    for a, b, n, c, v in ((32, 0, 32, 1, 0), (64, 32, 32, 2, 0), (64, 0, 64, 0, 1), (96, 64, 32, 1, 1), (96, 0, 32, 2, 1)):
-        (cp if v else ac)(R("g3", c, c + 1, slice(a, a + n)), R("cb", 191, 192, slice(b, b + n)))
-    tt(R("V1"), ind(R("identC"), R("c2u")), R("V0"), A.add)
-    scan(R("g3", 4, 8), R("seg32", 1, 5), R("g3", 0, 4))
-    ts(R("cub"), R("cb"), R("g3", 7, 8), None, A.add)
-    wq(0)
-    turn(R("zu"), R("cub"))
-    wq(1)
-    scan(R("zv"), R("X"), R("zu"), 0.0, A.mult, A.max)
-    cp(R("sl", 0, 6), R("zv", 15, 192, every, 32))
-    ts(R("sl", 6, 12), R("zv", 31, 192, every, 32), 192.0, None, A.min)
-    scatter(R("pw"), R("sl", 0, 6), R("V1"))
-    tt(R("val"), ind(R("identR"), R("sl", 6, 12)), R("V1"), A.add)
+    scatter(R("w1"), at(), R("val1"))
+    qx(0)
+    turn(R("wt", P=QM), R("w1", 0, 192, QM))
+    tt(R("OU"), R("OH", 0, 4), R("cf", 22, 26), A.add)
+    for q in [rank] + frm[:FAV]:
+        tt(R("Fa", 0, 6, Qd[q]), R("wt", 0, 192, QM, 32), R("wt", 16, 192, QM, 32), A.add)
+    for q in frm[FAV:]:
+        ac(R("Fa", 0, 6, Qd[q]), R("Fa", 0, 6, QM))
+    qx(1)
+    turn(R("Ta"), R("Fa"))
+    qx(2)
+    dup = R("LM", 12, 16)
 
-    def fold(s, a, n, lists, extra, gaps):
-        def gap():
-            if gaps:
-                gaps.pop(0)()
+    n2 = R("PS", 3, 96, every, 16)
+    rest, vals = list(range(6)), ["V0"]
+
+    def gather():
+        wait("v", [left["ma"]])
+        for k, d in enumerate(frm):
+            cp(R("LM", 0, 12, Qd[d]), R("A1", 12 * k, 12 * k + 12, Qd[d]))
+        if not OPT[1]:
+            ac(R("UB"), ind(R("OU"), tl()))
+
+    def places():
+        for k, d in enumerate(frm):
+            ac(R("XV", 0, 96, Qd[d], 8), R("A2", 12 * k, 12 * k + 12, Qd[d]))
+        ac(R("XV", 0, 96, every, 16), R("XV", 0, 96, every, 16), bias=256.0 + XO - ZC)
+        iota(R("pw", 0, 480), [[0, 480]])
+        iota(R("identR", 192, 200), [[0, 8]], base=-1000)
+        for n in ("Fs", "Fp"):
+            iota(R(n), [[0, SCRATCH[n][1][1]]])
+
+    def hop1():
+        pickq(R("Q1"), R("QX"), R("stl"))
+        picks(R("S1"), R("SX"), R("stl"))
+        send(("qa", block("Q1")), codes=True)
+        send(("sa", block("S1")))
+
+    def loads():
+        D("y", R("ws", 1024, 2048), None, "dw1", inap=T.w[:, 1024:2048])
+        copy("W1", "P1", ZC, X1, "QX", "SX", "dq1")
+        wait("y", [left["qa"]])
+        copy("W2", "P2", ZC, X1, "QX", "SX", "dq2")
+        D("y", R("ws", 2048, 3072), None, "dw2", inap=T.w[:, 2048:3072])
+        copy("W2", "P2", 0, ZC, "W1", "P1", "dq3")
+
+    def value():
+        tt(R("val"), ind(R("identR"), R("sl", 6, 12)), R("V1"), A.max)
+        vals.append("val")
+
+    side = {"w": lambda: wq(rest.pop(0)), "q": hop1, "x": value, "g": gather, "U": lambda: cp(R("UB"), ind(R("OU"), tl())), "C": lambda: ac(R("identC"), idn(512), scale=oh[2], bias=col(19)), "e": lambda: ts(R("cu", 0, 12), R("cl", 0, 12), 24.0, None, A.min), "z": lambda: cp(R("Za"), ind(R("Ta"), dup)), "d": loads, "u": lambda: qx(3), "h": places, "t": lambda: turn(R("La"), R("Za")),
+            "l": lambda: ts(R("stl", 0, 12, every, 2), R("La", 0, 6), float(ZC), None, A.add),
+            "L": lambda: ts(R("stl", 1, 12, every, 2), R("La", 32, 38), float(ZC), None, A.add),
+            "c": lambda: ts(R("c2u"), n2, -512.0 * rank, 511.0, A.add, A.min),
+            "v": lambda: turn(R("V0"), R("XV")),
+            "1": lambda: tt(R("V1"), ind(R("identC"), R("c2u")), R("V0"), A.add),
+            "a": lambda: ts(R("sl", 6, 12, every, 2), R("zv", 31, 96, every, 32), 192.0, None, A.min),
+            "A": lambda: ts(R("sl", 7, 12, every, 2), R("zv", 127, 192, every, 32), 192.0, None, A.min),
+            "y": lambda: scatter(R("pw"), R("sl", 0, 6), R("val"))}
+
+    def count():
+        tt(R("GB"), ind(R("tba"), lo()), R("UB"), A.mult)
+        yield
+        turn(R("PT"), R("GB"))
+        yield
+        scan(R("PS"), R("seg16"), R("PT"), 0.0, A.min, A.add)
+        yield
+        ts(R("kw", 0, 24), R("PS", 3, 96, every, 4), 1.0 / 512, -255.5 / 512, A.mult, A.add)
+        yield
+        tt(R("X"), ind(R("kw", 0, 25), R("cu", 0, 12)), R("K"), A.not_equal)
+        yield
+        turn(R("XT"), R("X"))
+        yield
+        scan(R("cb"), R("one"), R("XT"), 0.0, A.add, A.subtract)
+        yield
+        for a, b, n, c, v in ((32, 0, 32, 1, 0), (64, 32, 32, 2, 0), (64, 0, 64, 0, 1), (96, 64, 32, 1, 1), (96, 0, 32, 2, 1)):
+            (cp if v or OPT[0] else ac)(R("g3", c, c + 1, slice(a, a + n)), R("cb", 191, 192, slice(b, b + n)))
+        ac(R("identR", 0, 192), idn(192), scale=col(11), bias=col(20))
+        yield
+        scan(R("g3", 4, 8), R("seg32", 1, 5), R("g3", 0, 4))
+        yield
+        ts(R("cub"), R("cb"), R("g3", 7, 8), None, A.add)
+        yield
+        turn(R("zu"), R("cub"))
+        yield
+        scan(R("zv"), R("X"), R("zu"), 0.0, A.mult, A.max)
+        yield
+        for a in range(2):
+            cp(R("sl", a, 6, every, 2), R("zv", 96 * a + 15, 96 * a + 96, every, 32))
+            yield
+        scatter(R("pw"), R("sl", 0, 6), R(vals[-1]))
+        yield
+
+    def fold(s, a, n, m, sums):
         F_, H_, G_, T_, U_, S_, Z_, L_ = [x + s for x in "FHGTUSZL"]
-        turn(R("T1", a, a + 32 * n), R("pw", a, a + 32 * n))
-        gap()
-        for j, k in enumerate(lists + extra):
-            c = n * j if j < len(lists) else 32 + n * (j - len(lists))
-            tt(R(F_, c, c + n), R("T1", a + k, a + 32 * n, every, 32), R("T1", a + 16 + k, a + 32 * n, every, 32), A.add)
-        gap()
+        w = 192 if s == "s" else 96
+        for c in range(a, a + 32 * n, w):
+            turn(R("T1", c, c + w), R("pw", c, c + w))
+            yield
+        for i, (c, d, st, k, step) in enumerate(sums):
+            tt(R(F_, c, d, every, st), R("T1", a + k, a + 32 * n, every, step), R("T1", a + 16 + k, a + 32 * n, every, step), A.add)
+            if s == "p" or i == len(sums) - 1:
+                yield
         for q in (1, 3, 0, 2):
-            (ac if q % 2 else cp)(R(H_, P=Qd[q]), R(F_, P=Qd[q ^ 1]))
-        gap()
+            (ac if q % 2 or s in OPT[2] else cp)(R(H_, P=Qd[q]), R(F_, P=Qd[q ^ 1]))
+        yield
         tt(R(G_), R(F_), R(H_), A.add)
-        gap()
+        yield
         turn(R(T_), R(G_))
         turn(R(U_, P=upper), R(G_, P=lower))
         turn(R(U_, P=lower), R(G_, P=upper))
-        gap()
-        tt(R(S_), R(T_), R(U_), A.add)
-        gap()
-        cp(R(Z_), ind(R(S_, 0, 32), dup))
-        gap()
+        yield
+        for o, b, c in ((16, 0, 32), (0, 0, 16), (48, 16, 32)):
+            tt(R(Z_, o, o + c - b), R(T_, b, c), R(U_, b, c), A.add)
+        if s == "p":
+            tt(R("Sp", 32, 64), R("Tp", 32, 64), R("Up", 32, 64), A.add)
+            ac(R("idt"), R("Sp", 32, 64), bias=-1.0)
+            D("y", None, R("idt", P=slice(9, 18)), "di0", outap=T.id[0:1, :])
+            D("y", None, R("idt", P=slice(0, 9)), "di1", outap=T.id[1:2, :])
+        yield
         turn(R(L_), R(Z_))
-        gap()
-        m = n * len(lists)
+        yield
         for h in range(2):
             ts(R("l" + s, h, 2 * m, every, 2), R(L_, 32 * h, 32 * h + m), float(ZC), None, A.add)
+        yield
+        if s == "s":
+            pickq(R("Q3"), R("QX"), R("ls", 0, 12))
+            picks(R("S3"), R("SX"), R("ls", 0, 12))
+            send(("qb", block("Q3")), codes=True)
+            yield
+            pickq(R("Q4"), R("W1", 0, X1), R("ls", 12, 24))
+            picks(R("S4"), R("P1", 0, X1), R("ls", 12, 24))
+            send(("sb", block("S3")), ("sc", block("S4")))
+            send(("qc", block("Q4")), codes=True)
+            yield
 
-    def nop():
-        pass
+    chain = {"m": count(), "s": fold("s", 0, 6, 12, [(6 * k, 6 * k + 6, 1, 8 * k, 32) for k in range(2)]),
+             "p": fold("p", 192, 9, 27, [(c, c + 9, 1, k, 32) for c, k in ((0, 0), (9, 8), (18, 2), (32, 3), (41, 4))])}
+    for s in WEAVE.replace(" ", ""):
+        if s in side:
+            side[s]()
+        else:
+            next(chain[s])
 
-    fold("s", 0, 6, [0, 1], [], [])
-    pickq(R("Q3"), R("QX"), R("ls", 0, 12))
-    picks(R("S3"), R("SX"), R("ls", 0, 12))
-    send(("qb", block("Q3")), codes=True)
-    pickq(R("Q4"), R("W1", 0, X1), R("ls", 12, 24))
-    picks(R("S4"), R("P1", 0, X1), R("ls", 12, 24))
-    send(("sb", block("S3")), ("sc", block("S4")))
-    send(("qc", block("Q4")), codes=True)
-    scatter(R("pw"), R("sl", 0, 6), R("val"))
-    wq(2)
-    fold("p", 192, 9, [0, 1, 2], [3, 4], [nop, nop, lambda: wq(3), nop, nop, lambda: wq(4), nop, lambda: wq(5)])
-    ac(R("idt"), R("Sp", 32, 64), bias=-1.0)
-    D("y", None, R("idt", P=slice(9, 18)), "di0", outap=T.id[0:1, :])
-    D("y", None, R("idt", P=slice(0, 9)), "di1", outap=T.id[1:2, :])
-
-    for i, (q, s, w, p, l) in enumerate((("G2", "H2", "QX", "SX", 36), ("G1", "H1", "W1", "P1", 0), ("G0", "H0", "W2", "P2", 18))):
+    def products(i):
+        q, s, w, p, l = (("G2", "H2", "QX", "SX", 36), ("G1", "H1", "W1", "P1", 0), ("G0", "H0", "W2", "P2", 18))[i]
         for h, (a, b) in enumerate(PARTS):
             lst = R("lp", l + a // 16, l + b // 16)
             pickq(R(q, a, b), R(w), lst)
@@ -512,10 +543,16 @@ def rank_program(g, core, T, topo):
                 out = R("ps", d, d + b - a)
                 E("t", [R(q, a, b), R(s, a, b), R("WQ", c, c + 128), R("WS", c, c + 128)], [out] if i == 2 else [],
                   lambda e: e.matmul_mx(ap(out), ap(R("WQ", c, c + 128)), ap(R("WS", c, c + 128)), ap(R(q, a, b)), ap(R(s, a, b)), i == 0, i == 2))
-    for h, (a, b) in enumerate(PARTS):
+    def store(h):
+        a, b = PARTS[h]
         cp(R("ysb", a, b), R("ps", 512 * h, 512 * h + b - a))
         ac(R("ysb", M + a, M + b), R("ps", 1024 + 512 * h, 1024 + 512 * h + b - a))
         D("y", None, R("ysb", a, b), "dy0", h == 1, outap=T.y[:, a:b])
         D("y", None, R("ysb", M + a, M + b), "dy1", h == 1, outap=T.y[:, M + a:M + b])
+
+    for i in range(3):
+        products(i)
+    for h in range(2):
+        store(h)
 
     wait("g", [(q, cnt[q]) for q in ("v", "s", "t", "g")] + [left[h] for h in CALLS] + [(s, dsum[s]) for s in DMAS] + arrivals)

from concourse.bass import DstId, RemoteDMATransfer
from concourse.mybir import dt, AluOpType as A, ActivationFunctionType as AF

N, V, M, O = 4, 192, 288, 2
C = 64
ZC = 192
XO = 200
X1 = XO + 512
R0 = 123
PARTS = ((0, 128), (128, 288))
WEAVE = "zutglLqdhC memmmmvmcmm1mmmmmmamA sxssysspspspspss ppppwpwpwpwpwpwp"
FAV = 3
OPT = (0, 0, "")
TB = 768
F, I, U, B, H = "float32", "int32", "uint16", "bfloat16", "float16"
Q8, S8 = "float8_e4m3fn_x4", "uint8"


def _sb(w, d):
    return ("sbuf", [128, w], d)


SCRATCH = {
    "tba": _sb(1024, I), "land": ("dram", [4, 128, 8], I), "sb": _sb(40, I),
    "seg16": _sb(96, F), "OU": _sb(4, F), "UB": _sb(96, F), "PS": _sb(96, F), "A2": _sb(36, B), "MP": _sb(12, B),
    "xs": _sb(4 * 520, B), "ws": _sb(3072, B),
    "QX": _sb(X1, Q8), "SX": _sb(X1, S8), "W1": _sb(X1 + 192, Q8), "P1": _sb(X1 + 192, S8), "W2": _sb(X1 + 192, Q8), "P2": _sb(X1 + 192, S8),
    "WQ": _sb(768, Q8), "WS": _sb(768, S8), "OH": _sb(16, F),
    "Q1": _sb(192, Q8), "S1": _sb(192, S8), "Q3": _sb(192, Q8), "S3": _sb(192, S8), "Q4": _sb(192, Q8), "S4": _sb(192, S8),
    "G0": _sb(288, Q8), "H0": _sb(288, S8), "G1": _sb(288, Q8), "H1": _sb(288, S8), "G2": _sb(288, Q8), "H2": _sb(288, S8),
    "pI": _sb(2, I), "ci": _sb(8, I), "cf": _sb(32, F), "ident": _sb(X1, F), "identC": _sb(512, F), "identR": _sb(200, F),
    "seg32": _sb(192, B), "one": _sb(192, B), "K": _sb(192, F), "cl": _sb(40, F), "cu": _sb(16, U),
    "l0": _sb(36, I), "lf": _sb(72, F), "ul": _sb(40, U), "b2": _sb(6, I),
    "GA": _sb(192, I), "GT": _sb(192, I), "eqa": _sb(192, B), "cua": _sb(192, H), "za": _sb(192, H), "zt": _sb(192, H), "zs": _sb(192, H),
    "E1": _sb(6, F), "A1": _sb(36, U), "val1": _sb(96, F), "w1": _sb(384, F), "wt": _sb(192, F),
    "Fa": _sb(32, F), "Ta": _sb(32, F), "Za": _sb(64, F), "La": _sb(64, F), "stl": _sb(12, U),
    "GB": _sb(96, F), "PT": _sb(96, F), "kw": _sb(32, I), "c2u": _sb(6, U), "vi": _sb(12, I),
    "XV": _sb(96, F), "V0": _sb(96, F), "V1": _sb(96, F), "val": _sb(96, F),
    "X": _sb(192, B), "XT": _sb(192, B), "cb": _sb(192, B), "g3": _sb(8, F), "cub": _sb(192, H), "zu": _sb(192, H), "zv": _sb(192, H),
    "sl": _sb(12, U), "pw": _sb(1280, F), "T1": _sb(480, F),
    "Fs": _sb(32, F), "Hs": _sb(32, F), "Gs": _sb(32, F), "Ts": _sb(32, F), "Us": _sb(32, F), "Ss": _sb(32, F), "Zs": _sb(64, F), "Ls": _sb(64, F), "ls": _sb(24, U),
    "Fp": _sb(64, F), "Hp": _sb(64, F), "Gp": _sb(64, F), "Tp": _sb(64, F), "Up": _sb(64, F), "Sp": _sb(64, F), "Zp": _sb(64, F), "Lp": _sb(64, F), "lp": _sb(54, U),
    "idt": _sb(32, F), "ysb": _sb(576, F),
    "ps": ("psum", [128, 2048], F),
}
LISTS = {"la": (0, 12), "LM": (12, 28)}
DMAS = ["dnx", "dst", "dx", "dx1", "dw0", "dw1", "dw2", "dto", "dtr", "dq1", "dq2", "dq3", "dy0", "dy1", "di0", "di1"]
HOPS = ("nt", "ma", "mp", "qa", "sa", "qb", "qc", "sb", "sc")
CALLS = ("nt", "ma", "mp", "qa", "sa", "qb", "qc", "sb")
SEMAPHORES = ["v", "s", "t", "g"] + DMAS + [n + str(k) for n in HOPS for k in range(N - 1)] + ["l" + n for n in CALLS]


def plan(topo, src, cores):
    dsts = [c for c in cores if c != src]
    off = [c for c in dsts if topo.chip(c) != topo.chip(src)]
    on = [c for c in dsts if topo.chip(c) == topo.chip(src)]
    out, used = {}, []
    for grp in (off, on):
        if not grp:
            continue
        free = [e for e in topo.engines(src, grp[0]) if e not in used]
        w = 1
        while 2 * w * len(grp) <= len(free):
            w *= 2
        for i, c in enumerate(grp):
            out[c] = free[w * i:w * i + w]
        used = used + [e for c in grp for e in out[c]]
    return out


def rank_program(g, core, T, topo):
    rank = T.rank_of(core)
    if rank is None:
        return
    cores = list(T.cores)
    to = [(rank + 1 + k) % N for k in range(N - 1)]
    frm = [(rank - 1 - k) % N for k in range(N - 1)]
    eng = {"v": g.vector, "s": g.scalar, "t": g.tensor, "g": g, "y": g.sync}
    cnt = {q: 0 for q in eng}
    seen, writers, readers, dsum, pend, left = {}, {}, {}, {}, {}, {}
    Qd = [slice(32 * q, 32 * q + 32) for q in range(4)]
    lower, upper, every = slice(0, 64), slice(64, 128), slice(0, 128)
    QM, q3 = Qd[rank], Qd[3]

    def R(name, a=0, b=None, P=every, st=1):
        if name in LISTS:
            return ("ul", P.start, P.stop, LISTS[name][0] + a, LISTS[name][0] + (LISTS[name][1] if b is None else b), st)
        return (name, P.start, P.stop, a, SCRATCH[name][1][1] if b is None else b, st)

    def ind(win, off):
        return ("ind", win, off)

    def ap(x):
        if x[0] == "ind":
            return ap(x[1]).indirect(ap(x[2]))
        if x[0] == "land":
            return T.land[x[3]]
        if x[5] == 1:
            return T[x[0]][x[1]:x[2], x[3]:x[4]]
        return T[x[0]][x[1]:x[2], x[3]:x[4]:x[5]]

    def flat(xs):
        out = []
        for x in xs:
            if isinstance(x, tuple):
                out += flat(x[1:]) if x[0] == "ind" else [x]
        return out

    def meet(x, y):
        if x[1] >= y[2] or y[1] >= x[2] or x[3] >= y[4] or y[3] >= x[4]:
            return False
        return not (x[5] == y[5] and (x[3] - y[3]) % x[5])

    def inside(x, y):
        return y[1] <= x[1] and x[2] <= y[2] and y[3] <= x[3] and x[4] <= y[4] and (y[5] == 1 or y == x)

    def wait(q, toks):
        need = {}
        for sem, val in toks:
            if val > seen.get((q, sem), 0):
                need[sem] = max(need.get(sem, 0), val)
        for sem in need:
            eng[q].wait_ge(T.sem[sem], need[sem])
            seen[(q, sem)] = need[sem]

    def deps(q, rs, ws):
        toks = []
        for x in rs + ws:
            toks += [t for y, t in writers.get(x[0], []) if meet(x, y)]
        for x in ws:
            toks += [t for y, t in readers.get(x[0], []) if meet(x, y) and t[0] != q]
        wait(q, toks)

    def done(tok, rs, ws):
        for x in rs:
            readers.setdefault(x[0], []).append((x, tok))
        for x in ws:
            writers[x[0]] = [e for e in writers.get(x[0], []) if not inside(e[0], x)] + [(x, tok)]
            readers[x[0]] = [e for e in readers.get(x[0], []) if not inside(e[0], x)]

    def E(q, rs, ws, fn):
        rs, ws = flat(rs), flat(ws)
        deps(q, rs, ws)
        fn(eng[q]).then_inc(T.sem[q], 1)
        cnt[q] += 1
        done((q, cnt[q]), rs, ws)

    def D(q, out, in_, sem, fin=True, outap=None, inap=None):
        rs, ws = flat([in_]), flat([out])
        deps(q, rs, ws)
        eng[q].dma_start(ap(out) if outap is None else outap, ap(in_) if inap is None else inap).then_inc(T.sem[sem], 16)
        dsum[sem] = dsum.get(sem, 0) + 16
        pend.setdefault(sem, []).append((rs, ws))
        if fin:
            for rs, ws in pend.pop(sem):
                done((sem, dsum[sem]), rs, ws)

    def u8(v):
        return v.bitcast(dt.uint8)

    def u32(v):
        return v.bitcast(dt.uint32)

    land = {"ma": ("A1", 0, 12), "mp": ("A2", 0, 12), "qa": ("W1", 0, C), "sa": ("P1", 0, C), "qb": ("W1", X1, C), "sb": ("P1", X1, C), "qc": ("W2", X1, C), "sc": ("P2", X1, C)}

    def landed(h, k, sender):
        if h == "nt":
            return R("land", sender, sender + 1)
        n, a, w = land[h]
        return R(n, a + w * k, a + w * k + w)

    def share(src, dst, h):
        es = plan(topo, src, cores)
        if h in ("nt", "ma", "mp"):
            return es[dst][:min(len(e) for e in es.values())]
        es = es[dst]
        return es[:len(es) // 2] if h == "sb" else es[len(es) // 2:] if h == "sc" else es

    def send(*parts, codes=False):
        deps("g", flat([src(k) for h, src in parts for k in range(N - 1)]), [])
        tr, n = [], 0
        for h, src in parts:
            for k, d in enumerate(to):
                rid, pid, _ = topo.addr(cores[d])
                es = share(core, cores[d], h)
                n += len(es)
                s, t = ap(src(k)), ap(landed(h, k, rank))
                tr.append(RemoteDMATransfer(dst_ids=[DstId(rid=rid, pnc=pid)], dma_engine_mask=sum(1 << e for e in es),
                                            remote_sem=T.sem[h + str(k)], srcs=[u8(s) if codes else s], dsts=[u8(t) if codes else t]))
        left[parts[0][0]] = ("l" + parts[0][0], n)
        g.remote_dma_fused(tr, local_sem=T.sem["l" + parts[0][0]])

    def block(n, w=C):
        return lambda k: R(n, w * k, w * k + w)

    arrivals = []
    for h in HOPS:
        for k, d in enumerate(frm):
            tok = (h + str(k), len(share(cores[d], core, h)))
            arrivals.append(tok)
            x = landed(h, k, d)
            writers.setdefault(x[0], []).append((x, tok))

    def sc_(x):
        return ap(x) if isinstance(x, tuple) else x

    def ts(out, in0, s1, s2, o1, o2=None):
        if o2 is None:
            E("v", [in0, s1], [out], lambda e: e.tensor_scalar(ap(out), ap(in0), sc_(s1), None, o1))
        else:
            E("v", [in0, s1, s2], [out], lambda e: e.tensor_scalar(ap(out), ap(in0), sc_(s1), sc_(s2), o1, o2))

    def tt(out, a, b, op):
        E("v", [a, b], [out], lambda e: e.tensor_tensor(ap(out), ap(a), ap(b), op))

    def cp(out, in_):
        E("v", [in_], [out], lambda e: e.tensor_copy(ap(out), ap(in_)))

    def scatter(win, off, val):
        E("v", [off, val], [win], lambda e: e.tensor_copy(ap(win).indirect(ap(off)), ap(val)))

    def fill(out, c):
        E("v", [], [out], lambda e: e.memset(ap(out), c))

    def scan(out, d0, d1, init=0.0, o0=A.mult, o1=A.add):
        E("v", [d0, d1, init], [out], lambda e: e.tensor_tensor_scan(ap(out), ap(d0), ap(d1), sc_(init), o0, o1))

    def turn(out, in_):
        E("v", [in_], [out], lambda e: e.transpose(ap(out), ap(in_)))

    def ac(out, in_, scale=None, bias=None, fn=None):
        f = fn or (AF.Copy if bias is None else AF.Identity)
        kw = {}
        if scale is not None:
            kw["scale"] = sc_(scale)
        if bias is not None:
            kw["bias"] = sc_(bias)
        E("s", [in_, scale, bias], [out], lambda e: e.activation(ap(out), ap(in_), f, **kw))

    def idn(n, P=every):
        return R("ident", XO, XO + n, P)

    def co(out, c):
        ac(out, idn(min(256, len(range(out[3], out[4], out[5]))), slice(out[1], out[2])), scale=0.0, bias=c)

    def iota(out, pattern, cm=0, flag=True, base=0):
        if flag:
            E("g", [], [out], lambda e: e.iota(ap(out), pattern, base, cm, allow_small_or_imprecise_dtypes=True))
        else:
            E("g", [], [out], lambda e: e.iota(ap(out), pattern, base, cm))

    def pickq(out, win, off):
        E("v", [win, off], [out], lambda e: e.tensor_copy(u32(ap(out)), u32(ap(win)).indirect(ap(off))))

    def picks(out, win, off):
        E("s", [win, off], [out], lambda e: e.activation(ap(out), ap(win).indirect(ap(off)), AF.Copy))

    def quant(q, s, in_):
        E("v", [in_], [q, s], lambda e: e.quantize_mx(ap(q), ap(s), ap(in_)))

    def col(i, P=every):
        return R("cf", i, i + 1, P)

    def qx(i):
        a = ZC + 130 * i
        quant(R("QX", a, a + 130), R("SX", a, a + 130), R("xs", 520 * i, 520 * i + 520))

    def wq(i):
        quant(R("WQ", 128 * i, 128 * i + 128), R("WS", 128 * i, 128 * i + 128), R("ws", 512 * i, 512 * i + 512))

    def copy(w, p, a, b, q, s, sem):
        D("y", R(w, a, b), R(q, a, b), sem, False, outap=u8(ap(R(w, a, b))), inap=u8(ap(R(q, a, b))))
        D("y", R(p, a, b), R(s, a, b), sem)

    g6, g7 = slice(96, 112), slice(112, 128)
    for i in range(2):
        fill(R("sb", 20 * i, 20 * i + 8, g6), 0)
    D("y", R("land", rank, rank + 1), None, "dto", inap=T.nx[:])
    for i, t in enumerate((T.st, T.bt)):
        D("ys"[i], R("sb", 20 * i + 2, 20 * i + 14, g7), None, "dst", False, inap=t[:])
    for i, t in enumerate((T.st, T.bt)):
        D("ys"[i], R("sb", 20 * i + 8, 20 * i + 20, g6), None, "dst", i == 1, inap=t[:])
    for p in range(R0, 128):
        D("sy"[p % 2 == 0], R("tba", P=slice(p, p + 1)), None, "dnx", p == 127, inap=T.nx[:])
    D("y", R("xs", 32, 1040), None, "dx", inap=T.x[:, 0:1008])
    D("y", R("xs", 1040, 2080), None, "dx1", inap=T.x[:, 1008:2048])
    iota(R("ci", 4, 6), [[128 - R0 + 1 + rank, 2]], 1, False)
    iota(idn(256), [[1, 256]])
    iota(R("cl", 22, 34), [[4, 2], [8, 3], [0, 2]], base=1)
    iota(R("tba", TB, 1024, slice(0, R0)), [[0, 1024 - TB]], 0, False, 4096)
    send(("nt", lambda k: R("land", rank, rank + 1)))

    pi = R("ci", 4, 5)
    r15, p31, qf, pf, e127, s1, s2, basea, da = col(0), col(1), col(2), col(4), col(5), col(6), col(7), col(8), col(9)
    fill(R("ul"), XO)
    ts(R("ci", 0, 1), pi, 15, None, A.bitwise_and)
    ts(R("ci", 1, 2), pi, 31, None, A.bitwise_and)
    ts(R("ci", 2, 3), pi, 5, None, A.arith_shift_right)
    ts(R("ci", 3, 4), R("ci", 5, 6), 3, None, A.bitwise_and)
    ts(e127, pi, 127.0, None, A.is_equal)
    cp(R("cf", 0, 5), R("ci", 0, 5))
    lo, tl, at, c0 = [(lambda P=every, a=a: R("LM", a, a + 6, P)) for a in (0, 6, 16, 22)]
    fill(R("xs", 0, 32), 0.0)
    fill(R("tba", 0, TB, slice(0, R0)), 4096)
    ac(s1, e127, scale=2.0 - 1.0 / 512, bias=1.0 / 512)
    ac(s2, e127, scale=255.5 / 512, bias=-255.5 / 512)
    ac(basea, pf, scale=64.0, bias=1.0 - 64 * R0)
    ac(da, e127, scale=-5.0, bias=col(3))
    ac(R("cl", 16, 22), idn(6), scale=16.0, bias=r15)
    ac(R("cl", 12, 14), idn(2), scale=0.0, bias=r15)
    ac(R("cl", 14, 16), idn(2), scale=0.0, bias=R("cl", 17, 18))
    ac(R("ident", XO + 256, X1), idn(256), bias=256.0)
    co(R("seg32"), 1.0)
    co(R("w1", 0, 192), 0.0)
    co(R("seg32", 0, 192, every, 32), 0.0)
    co(R("MP"), 0.0)
    co(R("Fa"), 0.0)

    st0, bt0 = R("sb", 2, 14, q3), R("sb", 22, 34, q3)
    la, lb = [R("l0", 12 * i, 12 * i + 12, q3) for i in range(2)]
    fb, fc, fd, fe = [R("lf", 12 * i, 12 * i + 12, q3) for i in range(4)]
    ts(la, st0, 3, None, A.arith_shift_right)
    ts(lb, bt0, 1, None, A.bitwise_and)
    ts(fb, st0, 2.0, None, A.mult)
    ts(fc, la, -1023.0 / 64, None, A.mult)
    tt(fd, fb, lb, A.add)
    ts(R("b2", P=q3), R("sb", 28, 34, q3), 1, None, A.arith_shift_right)
    tt(fe, fd, fc, A.add)
    ts(c0(QM), R("sb", 8, 14, q3), float(XO), None, A.add)
    for a in range(2):
        ts(R("la", a, 12, q3, 2), R("lf", 36 + 6 * a, 42 + 6 * a, q3), 64.0, None, A.mult)
    ts(R("OH"), idn(16), r15, None, A.is_equal)
    ts(R("GA"), ind(R("tba"), R("la")), s1, s2, A.mult, A.add)
    ac(R("val1"), ind(R("ident"), c0()), bias=float(XO - ZC))
    oh = [R("OH", i, i + 1) for i in range(16)]
    ac(col(16), oh[4], scale=0.5)
    ac(col(10), oh[5], scale=-1.0)
    ac(R("cf", 22, 26), idn(4), scale=col(16))
    turn(R("GT", P=q3), R("GA", P=q3))
    wait("y", [("v", cnt["v"])])
    D("y", R("ws", 0, 1024), None, "dw0", inap=T.w[:, 0:1024])
    for i in range(8):
        D("y", R("tba", P=slice(16 * i, 16 * i + 4)), R("land", 0, 4), "dtr", i == 7, inap=T.land[:])
    n2x, t1 = R("GT", 31, 192, q3, 32), R("GT", 27, 192, q3, 32)
    ea, eb, ec, ed = [R("lf", 48 + 6 * i, 54 + 6 * i, q3) for i in range(4)]
    ef, eg = R("l0", 24, 30, q3), R("l0", 30, 36, q3)
    ts(R("eqa", P=q3), R("GA", P=q3), col(9, q3), None, A.is_equal)
    ts(eg, n2x, 1023, None, A.bitwise_and)
    ts(ef, n2x, 4, 63, A.arith_shift_right, A.bitwise_and)
    scan(R("cua", P=q3), R("eqa", P=q3), R("eqa", P=q3), col(8, q3), A.max, A.add)
    tt(ea, eg, R("b2", P=q3), A.add)
    ts(ec, ef, -1023.0 / 64, None, A.mult)
    scan(R("za", P=q3), R("cua", P=q3), R("eqa", P=q3), 0.0, A.max, A.mult)
    tt(ed, ea, ec, A.add)
    cp(tl(QM), t1)
    turn(R("zt", P=q3), R("za", P=q3))
    ts(lo(QM), ed, 64.0, None, A.mult)
    send(("ma", lambda k: R("LM", 0, 12)))
    cp(R("LM", 12, 22), R("cl", 12, 22))
    scan(R("zs", P=q3), R("seg32", P=q3), R("zt", P=q3))
    ts(R("MP", 0, 12, QM, 2), eg, 0.5, -256.0, A.mult, A.add)
    ts(at(QM), R("zs", 31, 192, q3, 32), -2.0, None, A.add)
    ts(R("MP", 1, 12, QM, 2), R("zs", 31, 192, q3, 32), -2.0 - ZC, None, A.add)
    send(("mp", lambda k: R("MP")))
    iota(R("seg16"), [[0, 6], [8192, 16]])
    iota(R("kw", 24, 25), [[0, 1]], 0, False)

    ac(col(17), oh[0], scale=100.0, bias=col(10))
    co(R("K"), -1.0)
    ac(R("cl", 0, 12), R("cl", 22, 34), bias=col(17))
    co(R("K", 0, 192, every, 16), 0.0)
    co(R("K", 5, 192, every, 32), float(rank))
    for k in range(3):
        co(R("K", 8 - k, 192, every, 32), 4.0 * rank + to[k])
        co(R("K", 24 - k, 192, every, 32), 4.0 * frm[k] + rank)
    ac(col(14), r15, scale=-5.0, bias=1.0)
    ac(col(21), qf, bias=1.0)
    ac(col(19), oh[2], scale=float(XO - ZC))
    ac(col(11), oh[0], bias=oh[8])
    ac(col(18), p31, scale=6.0, bias=col(14))
    co(R("XV"), 0.0)
    ac(R("g3", 3, 4), r15, scale=-64.0, bias=511.0)
    ac(col(20), col(11), scale=1000.0 + X1 - ZC, bias=-1000.0)
    ac(R("XV", 0, 96, QM, 16), R("MP", 0, 12, QM, 2))
    ac(R("XV", 8, 96, QM, 16), R("lf", 6, 12, q3), scale=0.5, bias=float(XO - ZC))
    ac(R("XV", 4, 96, every, 16), idn(6), scale=0.0, bias=col(21))
    ac(R("XV", 3, 96, every, 16), idn(6), scale=16.0, bias=col(18))
    co(R("one"), 1.0)
    co(R("g3", 0, 3), 0.0)

    scatter(R("w1"), at(), R("val1"))
    qx(0)
    turn(R("wt", P=QM), R("w1", 0, 192, QM))
    tt(R("OU"), R("OH", 0, 4), R("cf", 22, 26), A.add)
    for q in [rank] + frm[:FAV]:
        tt(R("Fa", 0, 6, Qd[q]), R("wt", 0, 192, QM, 32), R("wt", 16, 192, QM, 32), A.add)
    for q in frm[FAV:]:
        ac(R("Fa", 0, 6, Qd[q]), R("Fa", 0, 6, QM))
    qx(1)
    turn(R("Ta"), R("Fa"))
    qx(2)
    dup = R("LM", 12, 16)

    n2 = R("PS", 3, 96, every, 16)
    rest, vals = list(range(6)), ["V0"]

    def gather():
        wait("v", [left["ma"]])
        for k, d in enumerate(frm):
            cp(R("LM", 0, 12, Qd[d]), R("A1", 12 * k, 12 * k + 12, Qd[d]))
        if not OPT[1]:
            ac(R("UB"), ind(R("OU"), tl()))

    def places():
        for k, d in enumerate(frm):
            ac(R("XV", 0, 96, Qd[d], 8), R("A2", 12 * k, 12 * k + 12, Qd[d]))
        ac(R("XV", 0, 96, every, 16), R("XV", 0, 96, every, 16), bias=256.0 + XO - ZC)
        iota(R("pw", 0, 480), [[0, 480]])
        iota(R("identR", 192, 200), [[0, 8]], base=-1000)
        for n in ("Fs", "Fp"):
            iota(R(n), [[0, SCRATCH[n][1][1]]])

    def hop1():
        pickq(R("Q1"), R("QX"), R("stl"))
        picks(R("S1"), R("SX"), R("stl"))
        send(("qa", block("Q1")), codes=True)
        send(("sa", block("S1")))

    def loads():
        D("y", R("ws", 1024, 2048), None, "dw1", inap=T.w[:, 1024:2048])
        copy("W1", "P1", ZC, X1, "QX", "SX", "dq1")
        wait("y", [left["qa"]])
        copy("W2", "P2", ZC, X1, "QX", "SX", "dq2")
        D("y", R("ws", 2048, 3072), None, "dw2", inap=T.w[:, 2048:3072])
        copy("W2", "P2", 0, ZC, "W1", "P1", "dq3")

    def value():
        tt(R("val"), ind(R("identR"), R("sl", 6, 12)), R("V1"), A.max)
        vals.append("val")

    side = {"w": lambda: wq(rest.pop(0)), "q": hop1, "x": value, "g": gather, "U": lambda: cp(R("UB"), ind(R("OU"), tl())), "C": lambda: ac(R("identC"), idn(512), scale=oh[2], bias=col(19)), "e": lambda: ts(R("cu", 0, 12), R("cl", 0, 12), 24.0, None, A.min), "z": lambda: cp(R("Za"), ind(R("Ta"), dup)), "d": loads, "u": lambda: qx(3), "h": places, "t": lambda: turn(R("La"), R("Za")),
            "l": lambda: ts(R("stl", 0, 12, every, 2), R("La", 0, 6), float(ZC), None, A.add),
            "L": lambda: ts(R("stl", 1, 12, every, 2), R("La", 32, 38), float(ZC), None, A.add),
            "c": lambda: ts(R("c2u"), n2, -512.0 * rank, 511.0, A.add, A.min),
            "v": lambda: turn(R("V0"), R("XV")),
            "1": lambda: tt(R("V1"), ind(R("identC"), R("c2u")), R("V0"), A.add),
            "a": lambda: ts(R("sl", 6, 12, every, 2), R("zv", 31, 96, every, 32), 192.0, None, A.min),
            "A": lambda: ts(R("sl", 7, 12, every, 2), R("zv", 127, 192, every, 32), 192.0, None, A.min),
            "y": lambda: scatter(R("pw"), R("sl", 0, 6), R("val"))}

    def count():
        tt(R("GB"), ind(R("tba"), lo()), R("UB"), A.mult)
        yield
        turn(R("PT"), R("GB"))
        yield
        scan(R("PS"), R("seg16"), R("PT"), 0.0, A.min, A.add)
        yield
        ts(R("kw", 0, 24), R("PS", 3, 96, every, 4), 1.0 / 512, -255.5 / 512, A.mult, A.add)
        yield
        tt(R("X"), ind(R("kw", 0, 25), R("cu", 0, 12)), R("K"), A.not_equal)
        yield
        turn(R("XT"), R("X"))
        yield
        scan(R("cb"), R("one"), R("XT"), 0.0, A.add, A.subtract)
        yield
        for a, b, n, c, v in ((32, 0, 32, 1, 0), (64, 32, 32, 2, 0), (64, 0, 64, 0, 1), (96, 64, 32, 1, 1), (96, 0, 32, 2, 1)):
            (cp if v or OPT[0] else ac)(R("g3", c, c + 1, slice(a, a + n)), R("cb", 191, 192, slice(b, b + n)))
        ac(R("identR", 0, 192), idn(192), scale=col(11), bias=col(20))
        yield
        scan(R("g3", 4, 8), R("seg32", 1, 5), R("g3", 0, 4))
        yield
        ts(R("cub"), R("cb"), R("g3", 7, 8), None, A.add)
        yield
        turn(R("zu"), R("cub"))
        yield
        scan(R("zv"), R("X"), R("zu"), 0.0, A.mult, A.max)
        yield
        for a in range(2):
            cp(R("sl", a, 6, every, 2), R("zv", 96 * a + 15, 96 * a + 96, every, 32))
            yield
        scatter(R("pw"), R("sl", 0, 6), R(vals[-1]))
        yield

    def fold(s, a, n, m, sums):
        F_, H_, G_, T_, U_, S_, Z_, L_ = [x + s for x in "FHGTUSZL"]
        w = 192 if s == "s" else 96
        for c in range(a, a + 32 * n, w):
            turn(R("T1", c, c + w), R("pw", c, c + w))
            yield
        for i, (c, d, st, k, step) in enumerate(sums):
            tt(R(F_, c, d, every, st), R("T1", a + k, a + 32 * n, every, step), R("T1", a + 16 + k, a + 32 * n, every, step), A.add)
            if s == "p" or i == len(sums) - 1:
                yield
        for q in (1, 3, 0, 2):
            (ac if q % 2 or s in OPT[2] else cp)(R(H_, P=Qd[q]), R(F_, P=Qd[q ^ 1]))
        yield
        tt(R(G_), R(F_), R(H_), A.add)
        yield
        turn(R(T_), R(G_))
        turn(R(U_, P=upper), R(G_, P=lower))
        turn(R(U_, P=lower), R(G_, P=upper))
        yield
        for o, b, c in ((16, 0, 32), (0, 0, 16), (48, 16, 32)):
            tt(R(Z_, o, o + c - b), R(T_, b, c), R(U_, b, c), A.add)
        if s == "p":
            tt(R("Sp", 32, 64), R("Tp", 32, 64), R("Up", 32, 64), A.add)
            ac(R("idt"), R("Sp", 32, 64), bias=-1.0)
            D("y", None, R("idt", P=slice(9, 18)), "di0", outap=T.id[0:1, :])
            D("y", None, R("idt", P=slice(0, 9)), "di1", outap=T.id[1:2, :])
        yield
        turn(R(L_), R(Z_))
        yield
        for h in range(2):
            ts(R("l" + s, h, 2 * m, every, 2), R(L_, 32 * h, 32 * h + m), float(ZC), None, A.add)
        yield
        if s == "s":
            pickq(R("Q3"), R("QX"), R("ls", 0, 12))
            picks(R("S3"), R("SX"), R("ls", 0, 12))
            send(("qb", block("Q3")), codes=True)
            yield
            pickq(R("Q4"), R("W1", 0, X1), R("ls", 12, 24))
            picks(R("S4"), R("P1", 0, X1), R("ls", 12, 24))
            send(("sb", block("S3")), ("sc", block("S4")))
            send(("qc", block("Q4")), codes=True)
            yield

    chain = {"m": count(), "s": fold("s", 0, 6, 12, [(6 * k, 6 * k + 6, 1, 8 * k, 32) for k in range(2)]),
             "p": fold("p", 192, 9, 27, [(c, c + 9, 1, k, 32) for c, k in ((0, 0), (9, 8), (18, 2), (32, 3), (41, 4))])}
    for s in WEAVE.replace(" ", ""):
        if s in side:
            side[s]()
        else:
            next(chain[s])

    def products(i):
        q, s, w, p, l = (("G2", "H2", "QX", "SX", 36), ("G1", "H1", "W1", "P1", 0), ("G0", "H0", "W2", "P2", 18))[i]
        for h, (a, b) in enumerate(PARTS):
            lst = R("lp", l + a // 16, l + b // 16)
            pickq(R(q, a, b), R(w), lst)
            picks(R(s, a, b), R(p), lst)
            for o in range(O):
                c, d = 128 * ((2 - i) * O + o), 512 * (2 * o + h)
                out = R("ps", d, d + b - a)
                E("t", [R(q, a, b), R(s, a, b), R("WQ", c, c + 128), R("WS", c, c + 128)], [out] if i == 2 else [],
                  lambda e: e.matmul_mx(ap(out), ap(R("WQ", c, c + 128)), ap(R("WS", c, c + 128)), ap(R(q, a, b)), ap(R(s, a, b)), i == 0, i == 2))
    def store(h):
        a, b = PARTS[h]
        cp(R("ysb", a, b), R("ps", 512 * h, 512 * h + b - a))
        ac(R("ysb", M + a, M + b), R("ps", 1024 + 512 * h, 1024 + 512 * h + b - a))
        D("y", None, R("ysb", a, b), "dy0", h == 1, outap=T.y[:, a:b])
        D("y", None, R("ysb", M + a, M + b), "dy1", h == 1, outap=T.y[:, M + a:M + b])

    for i in range(3):
        products(i)
    for h in range(2):
        store(h)

    wait("g", [(q, cnt[q]) for q in ("v", "s", "t", "g")] + [left[h] for h in CALLS] + [(s, dsum[s]) for s in DMAS] + arrivals)
